import numpy as np, ml_dtypes
CORES = [23,119,17,113]
N = 4
import mx_ref
BF = ml_dtypes.bfloat16
def gentries(a):
    return np.ascontiguousarray(a.reshape(8, 16, -1).transpose(0, 2, 1)).reshape(8, -1)
def gtable(e):
    e = np.asarray(e); return np.ascontiguousarray(e.reshape(8, -1, 16).transpose(0, 2, 1)).reshape(128, -1).astype(np.int32)
def gcols(t, e):
    v = np.concatenate([t.reshape(8, 16, -1, 4), np.zeros((8, 16, 1, 4), BF)], axis=2)
    return np.ascontiguousarray(np.stack([v[g][:, e[g]] for g in range(8)])).reshape(128, -1)
def tile(rs):
    return np.stack(rs, axis=2).reshape(128, -1).astype(BF)
def pick(q, e):
    c = np.concatenate([q[0].reshape(128, -1, 4), np.zeros((128, 1, 4), np.uint8)], axis=1); s = np.concatenate([q[1], np.ones((16, 1), np.uint8)], axis=1)
    return (np.ascontiguousarray(c[:, e].reshape(128, -1)), np.ascontiguousarray(s[:, e]))
def join(*qs):
    return (np.concatenate([q[0] for q in qs], axis=1), np.concatenate([q[1] for q in qs], axis=1))
def put(q, e, v):
    c, s = q[0].reshape(128, -1, 4).copy(), q[1].copy(); c[:, e] = v[0].reshape(128, -1, 4); s[:, e] = v[1]
    return (c.reshape(128, -1), s)
def pk(c, s):
    return (np.ascontiguousarray(c), mx_ref.live(s))
def emit(q):
    return q[0], q[1]
def packed(v, rng):
    q = [mx_ref.quantize(np.ascontiguousarray(v[r])) for r in range(N)]
    return np.stack([a for a, b in q]), np.stack([mx_ref.plane(b, rng) for a, b in q])
def values_of_codes():
    e, c = np.zeros((128, 128, 4), np.float32), np.zeros((128, 2, 4), np.uint8)
    e[np.arange(128), np.arange(128), 0] = 1
    c[:127, :, 0] = np.arange(256).reshape(2, 128).T[:127]
    return mx_ref.matmul(mx_ref.quantize(e.reshape(128, 512).astype(BF)), (c.reshape(128, 8), np.full((16, 2), 127, np.uint8))).T.reshape(-1).astype(np.float64)
CODE_VALUE, SCALE_VALUE = values_of_codes(), 2.0 ** (np.arange(256) - 127.0)
def decode(q):
    return (CODE_VALUE[q[0]].reshape(16, 8, -1, 4) * SCALE_VALUE[q[1]][:, None, :, None] + 0.0).reshape(128, -1).astype(np.float32)
def f(rng, *shape):
    return mx_ref.flush((rng.standard_normal(shape, dtype=np.float32) * np.exp2(rng.integers(-2, 3, shape[:-1] + (1,)))).astype(BF))
def wide(rng, *shape, cols=0):
    v = rng.standard_normal(shape, dtype=np.float32) * np.exp2(rng.integers(-12, 13, shape)).astype(np.float32)
    if cols: v *= np.repeat(np.exp2(rng.integers(-cols, cols + 1, shape[:-2] + (1, shape[-1] // 4))) * (rng.random(shape[:-2] + (1, shape[-1] // 4)) > 0.0625), 4, axis=-1).astype(np.float32)
    return mx_ref.flush(v.astype(BF))
C, K, R = 320, 192, 3
def numbers_of(rng):
    return np.array(f(rng, N, 128, 4 * C)), np.array(f(rng, N, 128, 512)), np.array(f(rng, N, 128, 512))
def operands(rng):
    return rng.integers(0, C, (N, 8, C))
def layers(rng, still=[]):
    w = np.array(f(rng, N, 128, 2048)).reshape(N, 8, 16, 4, 8, 16, 4)
    for i in still:
        w[:, :, i] = 0
        w[:, :, :, :, :, i] = 0
    return w
def clear(u):
    a = u.reshape(N, 128, 128, 4)
    for i in range(5): a[:, :, i::16] = 0
    return a
def given(rng, x, l, m, u, v, w):
    c, s = packed(np.ascontiguousarray(w).reshape(N, 128, 2048), rng)
    return {"x": x.reshape(N, 128, 4 * C).astype(BF), "l": np.stack([gtable(l[r]) for r in range(N)]), "m": np.stack([gtable(m[r]) for r in range(N)]), "u": u.reshape(N, 128, 512), "v": v, "wc": c, "ws": s}
def setup_inputs(rng):
    x, u, v = numbers_of(rng)
    return given(rng, x, operands(rng), operands(rng), u, v, layers(rng))
def setup_inputs_ties(rng):
    x, u, v = numbers_of(rng)
    x = x.reshape(N, 8, 16, C, 4)
    x[:, :, 0] = 0
    x[:, :, 0, :, 0] = np.exp2(rng.integers(0, 3, (N, 8, C))).astype(BF)
    x[:, :, 1] = rng.integers(-1, 2, (N, 8, C, 4)).astype(np.float32).astype(BF)
    a = clear(u)
    o = rng.permutation(N)
    for r in range(N):
        for h in range(0, 128, 16):
            a[r, h, h, 0] = 0.0 if r == o[0] else -1.0 if r == o[1] else 1.0
            for b in range(4): a[r, h + 1, h + 1 + b, b] = 1.0
    e = o[2]
    x[e, :, 8:] = 0
    x[e, :, 8, :, 0] = 1.96875
    for i in range(6):
        x[e, :, 9 + i, :, 0] = ((1 + 0.125 * rng.integers(0, 8, (8, C))) * 2.0 ** -(10 + i)).astype(np.float32).astype(BF)
        for h in range(0, 128, 16):
            a[e, h, h, 0] = 0.0
            a[e, h + 9 + i, h, 0] = 2.0 ** (10 + i)
    return given(rng, x, operands(rng), operands(rng), a, v, layers(rng, [0, 1, 8, 9, 10, 11, 12, 13, 14, 15]))
def setup_inputs_near(rng):
    x, u, v = numbers_of(rng)
    x = x.astype(np.float32).reshape(N, 8, 16, C, 4)
    x[:, :, 0] = 0
    x[:, :, 8:] = 0
    a = clear(u)
    o = rng.permutation(N) % 4
    for r in range(N):
        if o[r] < 3:
            s = rng.integers(0, 16, (8, C))
            x[r, :, 8] = ((s[:, :, None] >> np.arange(4)) & 1) * np.exp2(np.arange(4) - 23.0)
            x[r, :, 12] = rng.integers(-1, 2, (8, C, 4)) * 2.0 ** -16
        else:
            x[r, :, 10] = rng.integers(-1, 2, (8, C, 4)) * 2.0 ** -29
            x[r, :, 12, :, :2] = (rng.integers(0, 2, (8, C, 2)) * 2.0 - 1.0) * 2.0 ** -30
            x[r, :, 12, :, 2:] = rng.integers(-1, 2, (8, C, 2)) * 2.0 ** -29
        if o[r] < 2:
            x[r, :, 0, :, 0] = rng.integers(0, 2, (8, C)) * 2.0 - 1.0 if o[r] == 0 else -1.0
            x[r, :, 11, :, 0] = 2.0 ** -10
        for g in rng.permutation(8)[:4]:
            c = rng.integers(C)
            x[r, g, 8:, c] = 0
            x[r, g, 0, c, 0] = 2.0 ** 29 * rng.choice([-1.0, 1.0])
            x[r, g, 12, c] = 2.0 ** 29 * rng.choice([-1.0, 1.0], 4)
        k = 1.0 if o[r] == 0 else 2.0 ** -30
        for h in range(0, 128, 16):
            a[r, h, h, 0] = k
            if o[r] < 3:
                a[r, h + 8, h] = k
                a[r, h + 11, h, 0] = k
            else: a[r, h + 10, h] = (np.array([1.0, 1.125, 1.25, 1.5]) * k).astype(BF)
            for b in range(4): a[r, h + 12, h + 1 + b, b] = k
    return given(rng, x, operands(rng), operands(rng), a, v, layers(rng, [0, 8, 9, 10, 11, 12, 13, 14, 15]))
def setup_inputs_late(rng):
    x, u, v = numbers_of(rng)
    x = x.reshape(N, 8, 16, C, 4)
    x[:, :, 0] = (rng.permutation(N) % 2 * 2.0 - 1.0).astype(BF)[:, None, None, None]
    a = clear(u)
    for h in range(0, 128, 16):
        a[:, h, h] = 1.0
        for b in range(4): a[:, h, h + 1 + b, b] = 1.0
    return given(rng, x, operands(rng), operands(rng), a, v, layers(rng))
def setup_inputs_huge(rng):
    x, u, v = numbers_of(rng)
    o = rng.permutation(N)
    c = np.where(np.argsort(rng.random((N, C)), axis=1) < C // 4, 1.0, -1.0)[:, None, None, :, None] * 2.0 ** 30
    x = (0.6 + 0.09 * rng.random((N, 8, 16, C, 4))) * c
    x[o == 0] = (0.9375 + 0.0625 * rng.integers(0, 2, (1, 8, 16, C, 4))) * c[o == 0]
    a = 2.0 ** 30 * (1.0 - 0.1 * rng.random((N, 128, 8, 4)))
    a[o == 0] = 2.0 ** 30
    for r in range(N): a[r] *= (rng.permutation(8) % 2 * 2.0 - 1.0)[None, :, None]
    u = u.reshape(N, 128, 128, 4)
    u[:, :, ::16] = a.astype(np.float32).astype(BF)
    w = np.zeros((N, 128, 4, 128, 4), np.float32)
    i = np.arange(128)
    for b in range(4): w[:, i, b, i, b] = -2
    return given(rng, x.astype(np.float32), operands(rng), operands(rng), u, v, w.astype(BF))
def setup_inputs_spread(rng):
    x, u, v = numbers_of(rng)
    x = np.array(wide(rng, N, 128, 4 * C, cols=6)).reshape(N, 16, 8, C, 4)
    t = np.exp2(-rng.integers(8, 15, (N, 16, 8, C // 8, 4)).astype(np.float64)) * (1 + (2 * rng.integers(0, 64, (N, 16, 8, C // 8, 4)) + 1) * 2.0 ** -7)
    t[:, :, 0, :, 0] = 1.96875
    x[:, :, :, 3::8] = (t * rng.choice([-1.0, 1.0], t.shape)).astype(np.float32).astype(BF)
    l, m = 2 * rng.integers(0, C // 2, (N, 8, C)), 2 * rng.integers(0, C // 2, (N, 8, C))
    e = rng.permutation(N)
    l[e[0]], m[e[0]] = C - 1, 0
    l[e[1]] = m[e[1]]
    l[e[2]], m[e[2]] = np.arange(C), C - 1 - np.arange(C)
    l[e[3]], m[e[3]] = rng.integers(0, 2, (8, C)), rng.integers(0, 2, (8, C))
    return given(rng, x, l, m, u, v, layers(rng))
def check_inputs(d):
    b = []
    for k in ("x", "u", "v"):
        a = np.abs(d[k].astype(np.float32))
        if not (np.isfinite(a).all() and ((a == 0) | (a >= 2.0 ** -30) & (a <= 2.0 ** 30)).all()): b.append("a value of " + k)
    for k in ("l", "m"):
        if not ((d[k] >= 0) & (d[k] < C)).all(): b.append("an entry of " + k)
    none, least, most = [emit(mx_ref.quantize(np.full((128, 16), k, np.float32).astype(BF)))[1][0, 0] for k in (0.0, 2.0 ** -30, 2.0 ** 30)]
    for r in range(N):
        if ((d["wc"][r] == 0x7F) | (d["wc"][r] == 0xFF)).any(): b.append("wc: a code that is no number")
        s = mx_ref.live(d["ws"][r])
        if ((s != none) & ((s < least) | (s > most))).any(): b.append("ws: a scale out of range")
    return b
def reference(x, l, m, u, v, wc, ws):
    qu = [mx_ref.quantize(u[r]) for r in range(N)]
    lay = [pk(wc[r], ws[r]) for r in range(N)]
    first, second = [gentries(l[r]) for r in range(N)], [gentries(m[r]) for r in range(N)]
    now = [x[r] for r in range(N)]
    lanes = np.arange(8)[:, None]
    left, right = np.zeros((N, 8, K), np.int64), np.zeros((N, 8, K), np.int64)
    for t in range(R):
        own, packs = [], []
        for r in range(N):
            q = mx_ref.quantize(now[r])
            own.append(decode(q).astype(BF))
            s = mx_ref.matmul(qu[r], q) + np.float32(0.0)
            n = np.argsort(-s[::16], axis=1, kind="stable")[:, :K]
            a, b = first[r][lanes, n], second[r][lanes, n]
            word = np.stack([s[i::16] > 0 for i in range(1, 5)])
            wa, wb = word[:, lanes, a], word[:, lanes, b]
            straight = np.count_nonzero(wa == wa[:, :1], axis=0) + np.count_nonzero(wb == wb[:, :1], axis=0)
            crossed = np.count_nonzero(wb == wa[:, :1], axis=0) + np.count_nonzero(wa == wb[:, :1], axis=0)
            left[r] = np.where(crossed > straight, b, a)
            right[r] = np.where(crossed > straight, a, b)
            z = (gcols(own[r], left[r]).astype(np.float32) - gcols(own[r], right[r]).astype(np.float32)) * np.float32(0.5)
            packs.append(mx_ref.quantize(z.astype(BF)))
        for r in range(N):
            e = (r + 1 + t) % N
            h = mx_ref.quantize(tile([mx_ref.matmul(pick(lay[e], np.arange(128 * b, 128 * b + 128)), packs[r]) * np.float32(0.03125) for b in range(4)]))
            who = np.full((8, C), -1)
            for k in reversed(range(K)): who[np.arange(8), left[r][:, k]] = k
            now[r] = (own[r].astype(np.float32) + gcols(decode(h).astype(BF), who).astype(np.float32)).astype(BF)
    y, ol = np.zeros((N, 128, C), np.float32), np.zeros((N, 8, 2 * K), np.float32)
    oc, osc = np.zeros((N, 128, 4 * C), np.uint8), np.zeros((N, 16, C), np.uint8)
    for r in range(N):
        q = mx_ref.quantize(now[r])
        y[r] = mx_ref.matmul(mx_ref.quantize(v[r]), q)
        ol[r] = np.concatenate([left[r], right[r]], axis=1)
        oc[r], osc[r] = emit(q)
    return {"y": y, "ol": ol, "oc": oc, "osc": osc}

@@ -1,0 +1,462 @@
+from concourse.mybir import dt, AluOpType, ActivationFunctionType
+
+A = AluOpType
+F = ActivationFunctionType
+C, K, R, N = 320, 192, 3, 4
+H = C // 2
+BIG = 2.0 ** 90
+TINY = 2.0 ** -110
+NB = C // 16
+KB = K // 16
+TILE_W = [320, 256, 192, 128, 128]
+TILE_0 = [0, 320, 576, 768, 896]
+CODE_0 = [0, 320, 576, 832, 960]
+HB = KB // 2
+SEG_W = [16 * (c % HB + 1) for c in range(KB)]
+SEG_0 = [sum(SEG_W[:c]) for c in range(KB + 1)]
+JUNK_0 = [8 * c * (c - 1) for c in range(NB + 1)]
+ON_SCALAR = (19, 18, 17, 16, 15)
+ON_VECTOR = (14, 13, 12, 11, 10)
+QUANT_AFTER = {5: [0], 3: [1], 1: [2, 3, 4]}
+DHW = 208
+
+BF, F32, I32, U16, U8, X4 = "bfloat16", "float32", "int32", "uint16", "uint8", "float8_e4m3fn_x4"
+SCRATCH = {"ps": ("psum", [128, 4096], F32)}
+for _n, _w, _d in [
+        ("xt", 1280, BF), ("qx", 320, X4), ("sx", 320, U8),
+        ("ut", 512, BF), ("qu", 128, X4), ("su", 128, U8), ("qr", 128, X4), ("sr", 128, U8),
+        ("vt", 512, BF), ("qv", 128, X4), ("sv", 128, U8),
+        ("li", 20, I32), ("mi", 20, I32), ("l16", 20, U16), ("m16", 20, U16),
+        ("wq", 512, X4), ("wp", 512, U8), ("lq0", 512, X4), ("lp0", 512, U8), ("lq1", 512, X4), ("lp1", 512, U8),
+        ("lq2", 512, X4), ("lp2", 512, U8),
+        ("ci", 8, I32), ("cf", 16, F32), ("tm", 320, F32), ("jj", 320, F32), ("i1", 32, I32), ("i2", 32, I32), ("boi", 128, BF),
+        ("ei", 128, BF), ("k1", 320, F32), ("d0", 320, F32), ("mne", 320, BF), ("c16", 320, BF),
+        ("zz", 336, BF), ("et", 520, BF), ("qe", 512, X4), ("se", 512, U8), ("bot", 512, BF), ("qb", 128, X4), ("sb", 128, U8),
+        ("g0t", 512, BF), ("qg", 128, X4), ("sg", 128, U8),
+        ("u1", 320, F32), ("z", 320, F32), ("ft", 4096, BF), ("qf", 1088, X4), ("sf", 1088, U8),
+        ("dsum", 320, BF), ("sgn", 1600, BF), ("vj", 1280, BF), ("junk", 720, BF),
+        ("rsb", 20, F32), ("rc", 20, F32), ("r1", 20, F32), ("r2", 20, F32),
+        ("r3", 20, F32), ("rsc", 320, F32), ("r4", 20, F32), ("pos", 20, U16),
+        ("bw", 320, BF), ("gm", 320, BF), ("pp", 320, BF), ("lr", 320, BF), ("mr", 320, BF), ("win", 336, BF), ("tr", 448, BF),
+        ("tl", 512, BF), ("ql", 128, X4), ("sl", 128, U8), ("prod", 64, F32), ("dsc", 64, F32), ("m4", 64, F32), ("m4i", 64, F32),
+        ("y0", 64, F32), ("y1", 64, F32), ("lrf", 64, F32), ("lr16", 32, U16),
+        ("th", 1280, BF), ("tt", 640, BF), ("gr", 768, BF), ("mt", 768, BF), ("qm", 192, X4), ("sm", 192, U8),
+        ("ht", 768, BF), ("qh", 192, X4), ("sh", 192, U8), ("dh", 4 * DHW, BF), ("g23", 640, BF),
+        ("rowl", 192, F32), ("ee", SEG_0[KB], BF), ("md", SEG_0[HB], BF), ("kci", 8, F32), ("kp", 8, F32), ("kn", 8, F32),
+        ("es", SEG_0[KB], BF), ("eri", 32, F32), ("ert", 32, F32),
+        ("nl", 16, F32), ("of", 16, F32), ("o16", 12, U16), ("ww", 896, BF), ("kv", 192, BF),
+        ("wsc", 320, BF), ("who", 20, U16), ("rci", 20, F32),
+        ("g1l", 4, U16), ("g2l", 2, U16), ("endl", 2, U16), ("repi", 8, I32), ("repl", 8, U16), ("cpat", 4, F32),
+        ("rt", 64, F32), ("rtt", 64, F32), ("olr", 384, F32), ("ysb", 320, F32)]:
+    SCRATCH[_n] = ("sbuf", [128, _w], _d)
+
+NDMA = 24
+SEMAPHORES = ["cv", "cs", "ct", "cg", "arr0", "arr1", "arr2", "sent"] + ["d%d" % i for i in range(NDMA)]
+ENGINE_SEM = {"v": "cv", "s": "cs", "t": "ct", "g": "cg"}
+
+
+def plan(g, T, ops):
+    queue = {"v": g.vector, "s": g.scalar, "t": g.tensor, "g": g, "y": g.sync}
+    last_w, readers, known, ndma = {}, {}, {q: {} for q in queue}, 0
+    for i, o in enumerate(ops):
+        q = o["q"]
+        deps = set(o["after"])
+        for t in o["r"]:
+            if t in last_w:
+                deps.add(last_w[t])
+            if t[0] == "@":
+                deps.update(j for j in readers.get(t, []) if ops[j]["q"] != q)
+        for t in o["w"]:
+            if t in last_w and not (t[0] == "@" and q == "t"):
+                deps.add(last_w[t])
+            deps.update(readers.get(t, []))
+        for t in o["r"]:
+            readers.setdefault(t, []).append(i)
+        for t in o["w"]:
+            last_w[t], readers[t] = i, []
+        if o["kind"] == "dma":
+            o["key"] = "d%d" % ndma
+            ndma += 1
+        else:
+            o["key"] = q
+        o["waits"] = []
+        for j in sorted(deps, reverse=True):
+            d = ops[j]
+            if known[q].get(d["key"], -1) >= j:
+                continue
+            o["waits"].append(j)
+            d["inc"] = True
+            for k, val in d["clock"].items():
+                known[q][k] = max(known[q].get(k, -1), val)
+        o["clock"] = dict(known[q])
+        o["clock"][o["key"]] = i
+    count = {q: 0 for q in ENGINE_SEM}
+    for o in ops:
+        e = queue[o["q"]]
+        for j in o["waits"]:
+            e.wait_ge(T.sem[ops[j]["sem"]], ops[j]["val"])
+        for name, val in o["ext"]:
+            e.wait_ge(T.sem[name], val)
+        ins = o["fn"](e)
+        if o["kind"] == "dma":
+            o["sem"], o["val"] = o["key"], 16
+            ins.then_inc(T.sem[o["sem"]], 16)
+        elif o["kind"] == "op" and o.get("inc"):
+            count[o["q"]] += 1
+            o["sem"], o["val"] = ENGINE_SEM[o["q"]], count[o["q"]]
+            ins.then_inc(T.sem[o["sem"]], 1)
+    for o in ops:
+        if o["kind"] == "dma" and not o.get("inc"):
+            queue[o["q"]].wait_ge(T.sem[o["sem"]], 16)
+
+
+def rank_program(g, core, T, topo):
+    rank = T.rank_of(core)
+    if rank is None:
+        return
+    ops = []
+
+    def op(q, fn, r=(), w=(), kind="op", after=(), ext=()):
+        ops.append({"q": q, "fn": fn, "r": list(r), "w": list(w), "kind": kind, "after": list(after), "ext": list(ext)})
+        return len(ops) - 1
+
+    def dma(q, out, in_, r=(), w=()):
+        return op(q, lambda e: e.dma_start(out, in_), r, w, "dma")
+
+    def ts(out, in0, s1, s2, o0, o1, r, w):
+        if o1 is None:
+            return op("v", lambda e: e.tensor_scalar(out, in0, s1, None, o0), r, w)
+        return op("v", lambda e: e.tensor_scalar(out, in0, s1, s2, o0, o1), r, w)
+
+    def tt(out, a, b, o, r, w):
+        return op("v", lambda e: e.tensor_tensor(out, a, b, o), r, w)
+
+    def cp(out, a, r, w):
+        return op("v", lambda e: e.tensor_copy(out, a), r, w)
+
+    def scan(out, a, b, init, o0, o1, r, w):
+        return op("v", lambda e: e.tensor_tensor_scan(out, a, b, init, o0, o1), r, w)
+
+    def turn(out, a, r, w):
+        return op("v", lambda e: e.transpose(out, a), r, w)
+
+    def fill(ap, val, w):
+        return op("v", lambda e: e.memset(ap, val), (), w)
+
+    def quant(q, s, a, r, w):
+        return op("v", lambda e: e.quantize_mx(q, s, a), r, w)
+
+    def act(out, a, func, r, w, **kw):
+        return op("s", lambda e: e.activation(out, a, func, **kw), r, w)
+
+    def mm(b, n, lq, ls, rq, rs, r, start=True, stop=True, ext=()):
+        out = T.ps[:, 512 * b:512 * b + n]
+        return op("t", lambda e: e.matmul_mx(out, lq, ls, rq, rs, start, stop), r, ["@%d" % b], ext=ext)
+
+    def bank(b, a, n):
+        return T.ps[:, 512 * b + a:512 * b + n]
+
+    def iota(out, pattern, base, cm, w, r=(), small=True):
+        if small:
+            return op("g", lambda e: e.iota(out, pattern, base, cm, allow_small_or_imprecise_dtypes=True), r, w)
+        return op("g", lambda e: e.iota(out, pattern, base, cm), r, w)
+
+    sent, lands = [0], []
+    for t in range(R):
+        src = T.cores[(rank + 1 + t) % N]
+        lands.append(2 * len(topo.engines(src, core)))
+
+    def send(t, after=()):
+        dst = T.cores[(rank - 1 - t) % N]
+        rid, pid, _ = topo.addr(dst)
+        mask = topo.mask(core, dst)
+        sent[0] += 2 * len(topo.engines(core, dst))
+        arr = T.sem["arr%d" % t]
+        op("g", lambda e: e.remote_dma(T["lq%d" % t][:].bitcast(dt.uint8), T.wq[:].bitcast(dt.uint8), arr, T.sem.sent, pid, rid, mask),
+           ["wq"], (), "remote", after)
+        op("g", lambda e: e.remote_dma(T["lp%d" % t][:], T.wp[:], arr, T.sem.sent, pid, rid, mask), ["wp"], (), "remote")
+
+    PF, QF, GRP, E16, SG, NT, N160, QB, SQ2 = [T.cf[:, i:i + 1] for i in range(9)]
+    XA, XB = ["x0", "x1", "x2", "x3"], ["x0", "x1", "x2", "x4"]
+
+    def tail(h):
+        lo = 16 * (NB - 3 - 4 * h) if h < 4 else 16
+        n = 4 * (TILE_W[h] - lo)
+        return T.ft[:, 4 * (TILE_0[h] + lo):4 * (TILE_0[h] + lo) + n], n, ["f%d" % (4 * h + s) for s in range(4)]
+
+    dma("y", T.ut[:], T.u[:], (), ["ut"])
+    dma("y", T.xt[:], T.x[:], (), ["x3", "x4"])
+    dma("s", T.li[:], T.l[:], (), ["li"])
+    dma("s", T.mi[:], T.m[:], (), ["mi"])
+    dma("y", T.wq[:].bitcast(dt.uint8), T.wc[:], (), ["wq"])
+    dma("y", T.wp[:], T.ws[:], (), ["wp"])
+    dma("y", T.vt[:], T.v[:], (), ["vt"])
+
+    iota(T.ci[:, 0:1], [[0, 1]], 0, 1, ["ci0"], small=False)
+    iota(T.tm[:], [[0, NB], [1, 16]], 0, 0, ["tm"])
+    iota(T.i1[:], [[1024, 32]], 1024 * 128, -1024, ["i1"], small=False)
+    iota(T.boi[:], [[1, 8], [0, 16]], 0, 0, ["boi"])
+    iota(T.ei[:], [[1, 128]], 0, -1, ["ei"])
+    iota(T.repi[:], [[16, 8]], 0, 0, ["repi"], small=False)
+    iota(T.jj[:], [[1, C]], 0, 0, ["jj"])
+    iota(T.rci[:], [[16, NB]], 15, 0, ["rci"])
+    iota(T.rt[:, 0:16], [[32, 2], [192, 2], [1, 4]], 1, 0, ["rt0"])
+    iota(T.rt[:, 16:32], [[32, 2], [192, 2], [1, 4]], 17, 0, ["rt1"])
+    iota(T.rt[:, 32:64], [[16, 2], [32, 8], [192, 2]], 8, 0, ["rt2"])
+    iota(T.cpat[:], [[64, 4]], 0, 0, ["cpat"])
+    for h in (3, 4):
+        ap, n, tags = tail(h)
+        iota(ap, [[0, n]], 0, 0, tags)
+    iota(T.kci[:], [[16, 8]], 128, 0, ["kci"])
+    iota(T.m4i[:], [[0, 16], [1, 4]], 0, 0, ["m4i"])
+    send(0)
+    iota(T.kv[:], [[1, K]], 1, 0, ["kv"])
+    for c in range(KB):
+        iota(T.eri[:, c:c + 1], [[0, 1]], SEG_0[c + 1] - 1, 0, ["eri%d" % c])
+    iota(T.eri[:, KB:16], [[0, 16 - KB]], 0, 0, ["eri%d" % KB])
+    fill(T.zz[:], 0.0, ["zz"])
+    fill(T.et[:], 0.0, ["et"])
+    fill(NT, -TINY, ["nt"])
+    quant(T.qf[:, 768:896], T.sf[:, 768:896], T.et[:, 0:512], ["et"], ["qfz", "qf3"])
+    fill(N160, -160.0, ["n160"])
+    for h in range(3):
+        ap, n, tags = tail(h)
+        act(ap, T.zz[:, 0:n], F.Copy, ["zz"], tags)
+    act(T.rsb[:], T.zz[:, 0:20], F.Copy, ["zz"], ["rs%d" % c for c in range(NB)])
+    ts(T.ci[:, 1:2], T.ci[:, 0:1], 15, None, A.bitwise_and, None, ["ci0"], ["ci1"])
+    ts(T.ci[:, 2:3], T.ci[:, 0:1], 4, None, A.arith_shift_right, None, ["ci0"], ["ci2"])
+    ts(T.ci[:, 3:4], T.ci[:, 0:1], 16, None, A.bitwise_and, None, ["ci0"], ["ci3"])
+    cp(T.cf[:, 0:4], T.ci[:, 0:4], ["ci0", "ci1", "ci2", "ci3"], ["pf", "qf", "grp"])
+    ts(QB, QF, -BIG, None, A.mult, None, ["qf"], ["qbig"])
+    ts(SQ2, QF, 15.0, 2.0, A.is_equal, A.mult, ["qf"], ["sq2"])
+    ts(T.d0[:], T.tm[:], QF, -BIG, A.is_le, A.mult, ["tm", "qf"], ["d0"])
+    ts(T.i2[:], T.i1[:], 15 * 1024, None, A.bitwise_and, None, ["i1"], ["i2"])
+    act(T.k1[:], T.tm[:], F.Abs, ["tm", "qbig"], ["k1"], bias=QB, scale=BIG)
+    act(T.mne[:], T.k1[:], F.Sign, ["k1"], ["mne"])
+    ts(SG, SQ2, 1.0, None, A.subtract, None, ["sq2"], ["sgc"])
+    ts(T.c16[:, 0:32], T.i2[:], 1025.0, 1.0, A.subtract, A.min, ["i2"], ["c16"])
+    for a, n in ((32, 32), (64, 64), (128, 128), (256, 64)):
+        act(T.c16[:, a:a + n], T.c16[:, 0:n], F.Copy, ["c16"], ["c16"])
+    act(T.win[:], T.zz[:], F.Copy, ["zz"], ["win"])
+    for s in range(4):
+        ts(T.bot[:, s:512:4], T.boi[:], GRP, None, A.is_equal, None, ["boi", "grp"], ["bot%d" % s])
+    ts(T.et[:, 3:515:4], T.ei[:], 0.0, None, A.is_equal, None, ["ei"], ["et"])
+    quant(T.qb[:], T.sb[:], T.bot[:], ["bot%d" % s for s in range(4)], ["qb"])
+    cp(T.repl[:], T.repi[:], ["repi"], ["repl"])
+    for b in range(4):
+        quant(T.qe[:, 128 * b:128 * b + 128], T.se[:, 128 * b:128 * b + 128], T.et[:, 3 - b:515 - b], ["et"], ["qe%d" % b])
+    fill(T.md[:], 0.0, ["md"])
+    for c in range(1, HB):
+        iota(T.md[:, SEG_0[c]:SEG_0[c] + 1], [[0, 1]], 4, 0, ["me%d" % c], ["md"])
+    cp(T.l16[:], T.li[:], ["li"], ["l16"])
+    cp(T.m16[:], T.mi[:], ["mi"], ["m16"])
+    act(T.lr[:], T.jj[:].indirect(T.l16[:]), F.Identity, ["jj", "l16", "n160"], ["lr"], bias=N160)
+    quant(T.qu[:], T.su[:], T.ut[:], ["ut"], ["qu"])
+    fill(T.g0t[:], 0.0, ["g0t"])
+    cp(T.qr[:].bitcast(dt.uint32), T.qu[:].bitcast(dt.uint32).indirect(T.repl[:]), ["qu", "repl"], ["qr"])
+    act(T.sr[:], T.su[:].indirect(T.repl[:]), F.Copy, ["qu", "repl"], ["sr"])
+    ts(T.rc[:], T.rci[:], QF, E16, A.subtract, A.add, ["rci", "qf", "grp"], ["rc"])
+    fill(T.tl[:], 0.0, ["tl"])
+    act(T.mr[:], T.jj[:].indirect(T.m16[:]), F.Identity, ["jj", "m16", "n160"], ["mr"], bias=N160)
+
+    def late_constants(part):
+        if part == 0:
+            turn(T.rtt[:], T.rt[:], ["rt0", "rt1", "rt2"], ["rtt"])
+        if part == 1:
+            act(T.tr[:, 384:448], T.zz[:, 0:64], F.Copy, ["zz"], ["trc"])
+            act(T.m4[:], T.m4i[:], F.Sign, ["m4i"], ["m4"])
+            act(T.y0[:], T.zz[:, 0:64], F.Copy, ["zz"], ["y0a", "y0b"])
+            act(T.dh[:, K:4 * DHW:DHW], T.zz[:, 0:4], F.Copy, ["zz"], ["dhz"])
+        if part == 2:
+            ts(T.g1l[:], T.cpat[:], T.rtt[:, 0:1], None, A.add, None, ["cpat", "rtt"], ["g1l"])
+            ts(T.g2l[:], T.jj[:, 0:2], T.rtt[:, 32:33], None, A.add, None, ["jj", "rtt"], ["g2l"])
+        if part == 3:
+            ts(T.g0t[:, 0:512:4], T.tm[:, 0:128], PF, None, A.is_equal, None, ["tm", "pf"], ["g0t"])
+            ts(T.kp[:], T.kci[:], QF, 1.0 / 256, A.add, A.mult, ["kci", "qf"], ["kp"])
+            ts(T.kn[:], T.kci[:], QF, -1.0 / 256, A.add, A.mult, ["kci", "qf"], ["kn"])
+            quant(T.qg[:], T.sg[:], T.g0t[:], ["g0t"], ["qg"])
+            for c in range(HB):
+                act(T.md[:, SEG_0[c + 1] - 16:SEG_0[c + 1]], T.mne[:, 0:16], F.Identity, ["mne", "kp", "kn", "md"], ["md%d" % c],
+                    bias=T.kn[:, c:c + 1], scale=T.kp[:, c:c + 1])
+        if part == 4:
+            act(T.eri[:, 16:32], T.eri[:, 0:16], F.Copy, ["eri%d" % c for c in range(KB + 1)], ["erj"])
+        if part == 5:
+            turn(T.ert[:], T.eri[:], ["erj"], ["ert"])
+        if part == 6:
+            cp(T.endl[:, 0:1], T.ert[:, 0:1], ["ert"], ["endl"])
+        if part == 7:
+            quant(T.qv[:], T.sv[:], T.vt[:], ["vt"], ["qv"])
+
+    def slot(i, n):
+        h, s = divmod(i, 4)
+        a = 4 * TILE_0[h] + s
+        return T.ft[:, a:a + 4 * n - 3:4]
+
+    def qtile(h):
+        a, b, n = CODE_0[h], TILE_0[h], TILE_W[h]
+        quant(T.qf[:, a:a + n], T.sf[:, a:a + n], T.ft[:, 4 * b:4 * (b + n)], ["f%d" % (4 * h + s) for s in range(4)], ["qf%d" % h])
+        if h < 3:
+            n = max(n, 256)
+            mm(3, n - 128, T.qb[:], T.sb[:], T.qf[:, a + 128:a + n], T.sf[:, a + 128:a + n], ["qb", "qf%d" % h, "qfz"], h == 0, h == 2)
+        mm(1, 128, T.qb[:], T.sb[:], T.qf[:, a:a + 128], T.sf[:, a:a + 128], ["qb", "qf%d" % h], h == 0, h == 4)
+
+    def compare(c):
+        i, n = NB - c, 16 * c
+        ts(slot(i, n), bank(0, 0, n), T.z[:, n + 15:n + 16], None, A.is_lt, None, ["@0", "za", "zb"], ["f%d" % i])
+        if c not in ON_VECTOR:
+            act(T.junk[:, JUNK_0[c]:JUNK_0[c] + n], slot(i, n), F.Identity, ["f%d" % i], ["rs%d" % c, "jk%d" % c],
+                accum_out=T.rsb[:, c:c + 1])
+
+    def row_sum(c):
+        n, end = 16 * c, 256 * (c - ON_VECTOR[-1] + 1)
+        scan(T.vj[:, end - n:end], slot(NB - c, n), T.zz[:, 0:n], 0.0, A.add, A.add, ["f%d" % (NB - c), "zz"], ["vj%d" % c])
+
+    def quant_state():
+        quant(T.qx[:, 0:H], T.sx[:, 0:H], T.xt[:, 0:4 * H], XA, ["qx"])
+        quant(T.qx[:, H:C], T.sx[:, H:C], T.xt[:, 4 * H:4 * C], XB, ["qy"])
+
+    for t in range(R):
+        quant_state()
+        mm(3, H, T.qr[:], T.sr[:], T.qx[:, 0:H], T.sx[:, 0:H], ["qr", "sr", "qx"])
+        mm(7, H, T.qr[:], T.sr[:], T.qx[:, H:C], T.sx[:, H:C], ["qr", "sr", "qy"])
+        mm(2, C, T.qu[:], T.su[:], T.qx[:], T.sx[:], ["qu", "qx", "qy"])
+        mm(0, C, T.qr[:], T.sr[:], T.qx[:], T.sx[:], ["qr", "sr", "qx", "qy"])
+        mm(1, C, T.qr[:], T.sr[:], T.qx[:], T.sx[:], ["qr", "sr", "qx", "qy"])
+        tt(T.u1[:, 0:H], bank(3, 0, H), T.k1[:, 0:H], A.subtract, ["@3", "k1"], ["u1a"])
+        tt(T.u1[:, H:C], bank(7, 0, H), T.k1[:, H:C], A.subtract, ["@7", "k1"], ["u1b"])
+        for b in range(4):
+            mm(4 + b, C, T.qe[:, 128 * b:128 * b + 128], T.se[:, 128 * b:128 * b + 128], T.qx[:], T.sx[:], ["qe%d" % b, "qx", "qy"])
+        act(T.bw[:], bank(2, 0, C), F.Sign, ["@2", "nt"], ["bw"], bias=NT)
+        scan(T.z[:, 0:H], T.d0[:, 0:H], T.u1[:, 0:H], 0.0, A.add, A.max, ["d0", "u1a"], ["za"])
+        scan(T.z[:, H:C], T.d0[:, H:C], T.u1[:, H:C], 0.0, A.add, A.max, ["d0", "u1b"], ["zb"])
+        if t == 0:
+            late_constants(0)
+        if t == 1:
+            late_constants(7)
+        act(T.gm[:], T.bw[:].indirect(T.m16[:]), F.Copy, ["bw", "m16"], ["gm"])
+        tt(slot(0, C), T.z[:], bank(0, 0, C), A.is_ge, ["za", "zb", "@0"], ["f0"])
+        for x in range(len(ON_SCALAR) + 1):
+            if x < len(ON_SCALAR):
+                n = 16 * ON_SCALAR[x]
+                act(T.sgn[:, C * x:C * x + n], bank(1, 0, n), F.Sign, ["@1", "za", "zb"], ["sgn%d" % x],
+                    bias=T.z[:, n + 15:n + 16], scale=-1.0)
+            if x > 0:
+                c = ON_SCALAR[x - 1]
+                act(slot(NB - c, 16 * c), T.sgn[:, C * (x - 1):C * (x - 1) + 16 * c], F.Relu, ["sgn%d" % (x - 1)],
+                    ["f%d" % (NB - c), "rs%d" % c], accum_out=T.rsb[:, c:c + 1])
+        todo = [c for c in range(NB - 1, 0, -1) if c not in ON_SCALAR]
+        for x, c in enumerate(todo):
+            compare(c)
+            if x > 0 and todo[x - 1] in ON_VECTOR:
+                row_sum(todo[x - 1])
+            if x > 1 and todo[x - 2] == ON_VECTOR[-1]:
+                lo, n = ON_VECTOR[-1], len(ON_VECTOR)
+                cp(T.rsb[:, lo:lo + n], T.vj[:, 255:256 * n:256], ["vj%d" % y for y in ON_VECTOR], ["rs%d" % y for y in ON_VECTOR])
+            if x == 0:
+                scan(T.dsum[:], T.mne[:], slot(0, C), 0.0, A.mult, A.add, ["mne", "f0"], ["dsum"])
+                tt(T.pp[:], T.bw[:].indirect(T.l16[:]), T.gm[:], A.subtract, ["bw", "l16", "gm"], ["pp", "ppl", "ppm"])
+                pl = dma("y", T.pp[8:128:16, :], T.lr[8:128:16, :], ["lr"], ["ppl"])
+                pm = dma("y", T.pp[9:128:16, :], T.mr[9:128:16, :], ["mr"], ["ppm"])
+                if t == 0:
+                    send(1, [pl, pm])
+                    send(2)
+            if x == 1:
+                tt(T.r1[:], T.rc[:], T.dsum[:, 15:C:16], A.subtract, ["rc", "dsum"], ["r1"])
+            for h in QUANT_AFTER.get(c, []):
+                qtile(h)
+        for b in range(4):
+            act(T.th[:, C * b:C * b + C], bank(4 + b, 0, C), F.Copy, ["@%d" % (4 + b)], ["th%d" % b], scale=0.5)
+        if t == 0:
+            late_constants(1)
+        for b in range(2):
+            act(T.tt[:, C * b:C * b + C], bank(4 + b, 0, C), F.Copy, ["@%d" % (4 + b)], ["tt%d" % b])
+        act(T.ww[:, 0:C], T.zz[:, 0:C], F.Identity, ["zz"], ["ww"], bias=float(K + 1))
+        tt(T.r2[:], T.r1[:], T.rsb[:], A.subtract, ["r1"] + ["rs%d" % c for c in range(NB)], ["r2"])
+        scan(T.rsc[:, 128:C], T.c16[:, 128:C], bank(3, 0, C - 128), SG, A.mult, A.min, ["c16", "@3", "sgc"], ["rsd"])
+        ts(T.r3[:], T.r2[:], SG, None, A.mult, None, ["r2", "sgc"], ["r3"])
+        scan(T.rsc[:, 0:128], T.c16[:, 0:128], bank(1, 0, 128), SG, A.mult, A.min, ["c16", "@1", "sgc"], ["rsc"])
+        tt(T.r4[:], T.rsc[:, 15:C:16], T.r3[:], A.add, ["rsc", "rsd", "r3"], ["r4"])
+        if t == 0:
+            late_constants(2)
+        ts(T.pos[:], T.r4[:], SG, None, A.mult, None, ["r4", "sgc"], ["pos"])
+        cp(T.win[:].indirect(T.pos[:]), T.pp[:], ["pos", "pp", "ppl", "ppm"], ["win"])
+        if t == 0:
+            late_constants(3)
+        turn(T.tr[:, 0:K], T.win[:, 0:K], ["win"], ["tra"])
+        turn(T.tr[:, K:2 * K], T.win[:, 16:16 + K], ["win"], ["trb"])
+        TR = ["tra", "trb", "trc"]
+        cp(T.tl[:, 0:256:4], T.tr[:].indirect(T.g1l[:]), TR + ["g1l"], ["tl"])
+        quant(T.ql[:], T.sl[:], T.tl[:], ["tl"], ["ql"])
+        mm(0, 128, T.qg[:], T.sg[:], T.ql[:], T.sl[:], ["qg", "ql"])
+        ts(T.y1[:, 1:64:2], T.tr[:].indirect(T.g2l[:]), 160.0, None, A.add, None, TR + ["g2l"], ["y1o"])
+        tt(T.y0[:, 1:32:2], T.y1[:, 33:64:2], T.y1[:, 1:32:2], A.subtract, ["y1o"], ["y0a"])
+        tt(T.prod[:], bank(0, 0, 64), T.tl[:, 0:256:4], A.mult, ["@0", "tl"], ["prod"])
+        tt(T.y0[:, 33:64:2], T.y1[:, 1:32:2], T.y1[:, 33:64:2], A.subtract, ["y1o"], ["y0b"])
+        scan(T.dsc[:], T.m4[:], T.prod[:], 0.0, A.mult, A.add, ["m4", "prod"], ["dsc"])
+        ts(T.y1[:, 0:32:2], T.dsc[:, 3:64:4], 0.0, None, A.is_lt, None, ["dsc"], ["y1e"])
+        ts(T.y1[:, 32:64:2], T.dsc[:, 3:64:4], 0.0, None, A.is_lt, None, ["dsc"], ["y1f"])
+        scan(T.lrf[:], T.y0[:], T.y1[:], 0.0, A.mult, A.add, ["y0a", "y0b", "y1e", "y1f", "y1o"], ["lrf"])
+        cp(T.lr16[:], T.lrf[:, 1:64:2], ["lrf"], ["lr16"])
+        left, right = T.lr16[:, 0:KB], T.lr16[:, 16:16 + KB]
+        cp(T.rowl[:], T.jj[:].indirect(left), ["jj", "lr16"], ["rowl"])
+        for b in range(4):
+            w = T.th[:, C * b:C * b + C]
+            act(T.gr[:, K * b:K * b + K], w.indirect(right), F.Copy, ["th%d" % b, "lr16"], ["gr%d" % b])
+            tt(T.mt[:, b:4 * K:4], w.indirect(left), T.gr[:, K * b:K * b + K], A.subtract, ["th%d" % b, "lr16", "gr%d" % b], ["mt%d" % b])
+        if t == 0:
+            late_constants(4)
+        for c in range(KB):
+            a = K // 2 * (c // HB)
+            act(T.ee[:, SEG_0[c]:SEG_0[c + 1]], T.rowl[:, a:a + SEG_W[c]], F.Abs, ["rowl", "lrf"], ["ee%d" % c],
+                bias=T.lrf[:, 2 * c + 1:2 * c + 2], scale=-1.0)
+        quant(T.qm[:], T.sm[:], T.mt[:], ["mt0", "mt1", "mt2", "mt3"], ["qm"])
+        lq, lp = T["lq%d" % t], T["lp%d" % t]
+        for b in range(4):
+            mm(b, K, lq[:, 128 * b:128 * b + 128], lp[:, 128 * b:128 * b + 128], T.qm[:], T.sm[:], ["qm"],
+               ext=[("arr%d" % t, lands[t])] if b == 0 else ())
+            act(T.ht[:, b:4 * K:4], bank(b, 0, K), F.Copy, ["@%d" % b], ["ht%d" % b], scale=0.03125)
+        if t == 0:
+            late_constants(5)
+        ts(T.nl[:], T.lrf[:, 1:32:2], -1.0 / 1024, None, A.mult, None, ["lrf"], ["nl"])
+        for h in range(2):
+            a, n = SEG_0[HB * h], SEG_0[HB]
+            scan(T.es[:, a:a + n], T.md[:], T.ee[:, a:a + n], 2.0, A.add, A.min,
+                 ["md%d" % c for c in range(HB)] + ["me%d" % c for c in range(1, HB)] + ["ee%d" % c for c in range(HB * h, HB * h + HB)],
+                 ["es%d" % h])
+            if t == 0 and h == 0:
+                late_constants(6)
+        tt(T.of[:], T.es[:].indirect(T.endl[:, 0:1]), T.nl[:], A.min, ["es0", "es1", "endl", "nl"], ["of"])
+        ts(T.o16[:], T.of[:, 0:KB], -1024.0, None, A.mult, None, ["of"], ["o16"])
+        cp(T.ww[:].indirect(T.o16[:, HB:KB]), T.kv[:, K // 2:K], ["o16", "kv"], ["ww"])
+        quant(T.qh[:], T.sh[:], T.ht[:], ["ht0", "ht1", "ht2", "ht3"], ["qh"])
+        for b, bk in enumerate((4, 5, 0, 1)):
+            mm(bk, K, T.qe[:, 128 * b:128 * b + 128], T.se[:, 128 * b:128 * b + 128], T.qh[:], T.sh[:], ["qe%d" % b, "qh"])
+            act(T.dh[:, DHW * b:DHW * b + K], bank(bk, 0, K), F.Copy, ["@%d" % bk], ["dh%d" % b])
+        cp(T.ww[:].indirect(T.o16[:, 0:HB]), T.kv[:, 0:K // 2], ["o16", "kv"], ["ww"])
+        scan(T.wsc[:], T.c16[:], T.ww[:, 0:C], SG, A.mult, A.min, ["c16", "ww", "sgc"], ["wsc"])
+        ts(T.who[:], T.wsc[:, 15:C:16], SG, 1.0, A.mult, A.subtract, ["wsc", "sgc"], ["who"])
+        for b in (2, 3):
+            act(T.g23[:, C * (b - 2):C * (b - 1)], T.dh[:, DHW * b:DHW * b + K + 1].indirect(T.who[:]), F.Copy,
+                ["dh%d" % b, "dhz", "who"], ["g%d" % b])
+        if t == R - 1:
+            act(T.olr[:, 0:K], T.jj[:].indirect(left), F.Copy, ["jj", "lr16"], ["ol0"])
+            act(T.olr[:, K:2 * K], T.jj[:].indirect(right), F.Copy, ["jj", "lr16"], ["ol1"])
+            dma("y", T.ol[:], T.olr[0:128:16, :], ["ol0", "ol1"])
+        for b in (0, 1):
+            tt(T.xt[:, b:4 * C:4], T.dh[:, DHW * b:DHW * b + K + 1].indirect(T.who[:]), T.tt[:, C * b:C * b + C], A.add,
+               ["dh%d" % b, "dhz", "who", "tt%d" % b], ["x%d" % b])
+        tt(T.xt[:, 2:4 * C:4], bank(6, 0, C), T.g23[:, 0:C], A.add, ["@6", "g2"], ["x2"])
+        tt(T.xt[:, 3:4 * H:4], bank(7, 0, H), T.g23[:, C:C + H], A.add, ["@7", "g3"], ["x3"])
+        tt(T.xt[:, 4 * H + 3:4 * C:4], bank(7, H, C), T.g23[:, C + H:2 * C], A.add, ["@7", "g3"], ["x4"])
+
+    quant_state()
+    mm(0, H, T.qv[:], T.sv[:], T.qx[:, 0:H], T.sx[:, 0:H], ["qv", "qx"])
+    mm(1, H, T.qv[:], T.sv[:], T.qx[:, H:C], T.sx[:, H:C], ["qv", "qy"])
+    dma("y", T.oc[:], T.qx[:].bitcast(dt.uint8), ["qx", "qy"])
+    act(T.ysb[:, 0:H], bank(0, 0, H), F.Copy, ["@0"], ["ya"])
+    cp(T.ysb[:, H:C], bank(1, 0, H), ["@1"], ["yb"])
+    for k in range(4):
+        dma("y", T.osc[4 * k:4 * k + 4, :], T.sx[32 * k:32 * k + 4, :], ["qx", "qy"])
+    dma("s", T.y[:], T.ysb[:], ["ya", "yb"])
+    plan(g, T, ops)
+    g.wait_ge(T.sem.sent, sent[0])

@@ -1,3 +1,4 @@
+import numpy as np
 from concourse.mybir import dt, AluOpType, ActivationFunctionType
 
 A = AluOpType
@@ -8,17 +9,17 @@ BIG = 2.0 ** 90
 TINY = 2.0 ** -110
 NB = C // 16
 KB = K // 16
-TILE_W = [320, 256, 192, 128, 128]
-TILE_0 = [0, 320, 576, 768, 896]
-CODE_0 = [0, 320, 576, 832, 960]
-HB = KB // 2
+TILE_W = [320, 256, 192, 128, 64]
+TILE_0 = [0, 320, 576, 768, 896, 960]
+PARTS = 3
+HB = KB // PARTS
 SEG_W = [16 * (c % HB + 1) for c in range(KB)]
-SEG_0 = [sum(SEG_W[:c]) for c in range(KB + 1)]
-JUNK_0 = [8 * c * (c - 1) for c in range(NB + 1)]
+SEG_0 = [sum(SEG_W[:c]) + c for c in range(KB + 1)]
+SEG_ALL = SEG_0[HB] * 16 // HB
 ON_SCALAR = (19, 18, 17, 16, 15)
-ON_VECTOR = (14, 13, 12, 11, 10)
-QUANT_AFTER = {5: [0], 3: [1], 1: [2, 3, 4]}
-DHW = 208
+SCAN_FROM = 3
+STEP, LIFT = 512.0, 16384.0
+W = K + C
 
 BF, F32, I32, U16, U8, X4 = "bfloat16", "float32", "int32", "uint16", "uint8", "float8_e4m3fn_x4"
 SCRATCH = {"ps": ("psum", [128, 4096], F32)}
@@ -29,56 +30,88 @@ for _n, _w, _d in [
         ("li", 20, I32), ("mi", 20, I32), ("l16", 20, U16), ("m16", 20, U16),
         ("wq", 512, X4), ("wp", 512, U8), ("lq0", 512, X4), ("lp0", 512, U8), ("lq1", 512, X4), ("lp1", 512, U8),
         ("lq2", 512, X4), ("lp2", 512, U8),
-        ("ci", 8, I32), ("cf", 16, F32), ("tm", 320, F32), ("jj", 320, F32), ("i1", 32, I32), ("i2", 32, I32), ("boi", 128, BF),
-        ("ei", 128, BF), ("k1", 320, F32), ("d0", 320, F32), ("mne", 320, BF), ("c16", 320, BF),
-        ("zz", 336, BF), ("et", 520, BF), ("qe", 512, X4), ("se", 512, U8), ("bot", 512, BF), ("qb", 128, X4), ("sb", 128, U8),
+        ("ci", 8, I32), ("cf", 16, F32), ("tm", 320, BF), ("jj", 320, F32), ("boi", 128, BF),
+        ("ei", 128, BF), ("k1", 320, BF), ("d0", 160, BF), ("mne", 320, BF), ("c16", 320, BF),
+        ("zz", 520, BF), ("et", 520, BF), ("qe", 512, X4), ("se", 512, U8), ("bot", 512, BF), ("qb", 128, X4), ("sb", 128, U8),
         ("g0t", 512, BF), ("qg", 128, X4), ("sg", 128, U8),
-        ("u1", 320, F32), ("z", 320, F32), ("ft", 4096, BF), ("qf", 1088, X4), ("sf", 1088, U8),
-        ("dsum", 320, BF), ("sgn", 1600, BF), ("vj", 1280, BF), ("junk", 720, BF),
-        ("rsb", 20, F32), ("rc", 20, F32), ("r1", 20, F32), ("r2", 20, F32),
-        ("r3", 20, F32), ("rsc", 320, F32), ("r4", 20, F32), ("pos", 20, U16),
+        ("u1", 320, F32), ("z", 320, F32), ("ft", 3840, BF), ("qf", 1216, X4), ("sf", 1216, U8),
+        ("dsum", 320, BF), ("sgn", 2240, BF), ("vj", 3840, BF), ("junk", 3840, BF), ("rmask", 960, BF),
+        ("rsb", 20, F32), ("rc", 20, F32), ("r1", 20, F32), ("rsc", 320, F32), ("r4", 20, F32), ("pos", 20, U16),
         ("bw", 320, BF), ("gm", 320, BF), ("pp", 320, BF), ("lr", 320, BF), ("mr", 320, BF), ("win", 336, BF), ("tr", 448, BF),
-        ("tl", 512, BF), ("ql", 128, X4), ("sl", 128, U8), ("prod", 64, F32), ("dsc", 64, F32), ("m4", 64, F32), ("m4i", 64, F32),
-        ("y0", 64, F32), ("y1", 64, F32), ("lrf", 64, F32), ("lr16", 32, U16),
-        ("th", 1280, BF), ("tt", 640, BF), ("gr", 768, BF), ("mt", 768, BF), ("qm", 192, X4), ("sm", 192, U8),
-        ("ht", 768, BF), ("qh", 192, X4), ("sh", 192, U8), ("dh", 4 * DHW, BF), ("g23", 640, BF),
-        ("rowl", 192, F32), ("ee", SEG_0[KB], BF), ("md", SEG_0[HB], BF), ("kci", 8, F32), ("kp", 8, F32), ("kn", 8, F32),
-        ("es", SEG_0[KB], BF), ("eri", 32, F32), ("ert", 32, F32),
-        ("nl", 16, F32), ("of", 16, F32), ("o16", 12, U16), ("ww", 896, BF), ("kv", 192, BF),
-        ("wsc", 320, BF), ("who", 20, U16), ("rci", 20, F32),
+        ("tl", 512, BF), ("ql", 128, X4), ("sl", 128, U8), ("prod", 64, BF), ("dsc", 64, BF), ("m4", 64, BF),
+        ("y0", 48, F32), ("y1", 96, F32), ("lrf", 48, F32), ("lf16", 16, U16), ("rt16", 16, U16),
+        ("wn", 4 * W, BF), ("gl", 768, BF), ("mt", 768, BF), ("qm", 192, X4), ("sm", 192, U8),
+        ("ht", 768, BF), ("qh", 192, X4), ("sh", 192, U8),
+        ("rowl", 384, F32), ("ee", SEG_ALL, BF), ("md", SEG_0[KB], BF), ("kci", 8, F32), ("kp", 8, F32), ("kn", 8, F32),
+        ("es", SEG_ALL, BF), ("nl", 16, BF), ("th", 640, BF), ("tf", 640, BF), ("o16", 16, U16), ("ww", 896, F32),
+        ("wsc", 320, F32), ("who", 20, U16), ("rci", 20, F32),
         ("g1l", 4, U16), ("g2l", 2, U16), ("endl", 2, U16), ("repi", 8, I32), ("repl", 8, U16), ("cpat", 4, F32),
-        ("rt", 64, F32), ("rtt", 64, F32), ("olr", 384, F32), ("ysb", 320, F32)]:
+        ("rt", 96, F32), ("rtt", 96, F32), ("ysb", 320, F32)]:
     SCRATCH[_n] = ("sbuf", [128, _w], _d)
 
-NDMA = 24
+NDMA = 40
 SEMAPHORES = ["cv", "cs", "ct", "cg", "arr0", "arr1", "arr2", "sent"] + ["d%d" % i for i in range(NDMA)]
 ENGINE_SEM = {"v": "cv", "s": "cs", "t": "ct", "g": "cg"}
+ALL = slice(0, 128)
+
+
+def V(name, a=0, b=None, step=1, parts=ALL):
+    return (name, parts, slice(a, SCRATCH[name][1][1] if b is None else b, step), None, None)
+
+
+def col(name, a):
+    return V(name, a, a + 1)
+
+
+def by(win, off):
+    return win[:4] + (off,)
+
+
+def as_(v, d):
+    return v[:3] + (d, v[4])
+
+
+def bank(b, a, n):
+    return V("ps", 512 * b + a, 512 * b + n)
+
+
+def is_view(v):
+    return isinstance(v, tuple)
 
 
 def plan(g, T, ops):
     queue = {"v": g.vector, "s": g.scalar, "t": g.tensor, "g": g, "y": g.sync}
-    last_w, readers, known, ndma = {}, {}, {q: {} for q in queue}, 0
+    wrote = {n: np.full((1, 8) if n == "ps" else s[1], -1) for n, s in SCRATCH.items()}
+    read = {n: {} for n in SCRATCH}
+    known, ndma = {q: {} for q in queue}, 0
+
+    def at(v):
+        return (slice(0, 1), slice(v[2].start // 512, v[2].start // 512 + 1)) if v[0] == "ps" else (v[1], v[2])
+
     for i, o in enumerate(ops):
         q = o["q"]
-        deps = set(o["after"])
-        for t in o["r"]:
-            if t in last_w:
-                deps.add(last_w[t])
-            if t[0] == "@":
-                deps.update(j for j in readers.get(t, []) if ops[j]["q"] != q)
-        for t in o["w"]:
-            if t in last_w and not (t[0] == "@" and q == "t"):
-                deps.add(last_w[t])
-            deps.update(readers.get(t, []))
-        for t in o["r"]:
-            readers.setdefault(t, []).append(i)
-        for t in o["w"]:
-            last_w[t], readers[t] = i, []
         if o["kind"] == "dma":
             o["key"] = "d%d" % ndma
             ndma += 1
         else:
             o["key"] = q
+        reads = [v for v in o["r"] if is_view(v)]
+        reads += [v[4] for v in reads + o["w"] if v[4] is not None]
+        deps = set(o["after"])
+        for v in reads:
+            deps.update(np.unique(wrote[v[0]][at(v)]).tolist())
+            if v[0] == "ps":
+                deps.update(int(m[at(v)].max()) for k, m in read["ps"].items() if k != q)
+        for v in o["w"]:
+            if v[0] != "ps":
+                deps.update(np.unique(wrote[v[0]][at(v)]).tolist())
+            deps.update(int(m[at(v)].max()) for m in read[v[0]].values())
+        for v in reads:
+            read[v[0]].setdefault(o["key"], np.full(wrote[v[0]].shape, -1))[at(v)] = i
+        for v in o["w"]:
+            wrote[v[0]][at(v)] = i
+        deps.discard(-1)
+        deps.discard(i)
         o["waits"] = []
         for j in sorted(deps, reverse=True):
             d = ops[j]
@@ -116,51 +149,60 @@ def rank_program(g, core, T, topo):
         return
     ops = []
 
+    def ap(v):
+        if not is_view(v):
+            return v
+        x = T[v[0]][v[1], v[2]]
+        if v[3] is not None:
+            x = x.bitcast(v[3])
+        return x if v[4] is None else x.indirect(ap(v[4]))
+
     def op(q, fn, r=(), w=(), kind="op", after=(), ext=()):
-        ops.append({"q": q, "fn": fn, "r": list(r), "w": list(w), "kind": kind, "after": list(after), "ext": list(ext)})
+        ops.append({"q": q, "fn": fn, "r": list(r), "w": [v for v in w if is_view(v)], "kind": kind, "after": list(after), "ext": list(ext)})
         return len(ops) - 1
 
-    def dma(q, out, in_, r=(), w=()):
-        return op(q, lambda e: e.dma_start(out, in_), r, w, "dma")
+    def dma(q, out, in_):
+        return op(q, lambda e: e.dma_start(ap(out), ap(in_)), [in_], [out], "dma")
 
-    def ts(out, in0, s1, s2, o0, o1, r, w):
+    def ts(out, in0, s1, o0, s2=None, o1=None):
         if o1 is None:
-            return op("v", lambda e: e.tensor_scalar(out, in0, s1, None, o0), r, w)
-        return op("v", lambda e: e.tensor_scalar(out, in0, s1, s2, o0, o1), r, w)
+            return op("v", lambda e: e.tensor_scalar(ap(out), ap(in0), ap(s1), None, o0), [in0, s1], [out])
+        return op("v", lambda e: e.tensor_scalar(ap(out), ap(in0), ap(s1), ap(s2), o0, o1), [in0, s1, s2], [out])
 
-    def tt(out, a, b, o, r, w):
-        return op("v", lambda e: e.tensor_tensor(out, a, b, o), r, w)
+    def tt(out, a, b, o):
+        return op("v", lambda e: e.tensor_tensor(ap(out), ap(a), ap(b), o), [a, b], [out])
 
-    def cp(out, a, r, w):
-        return op("v", lambda e: e.tensor_copy(out, a), r, w)
+    def cp(out, a):
+        return op("v", lambda e: e.tensor_copy(ap(out), ap(a)), [a], [out])
 
-    def scan(out, a, b, init, o0, o1, r, w):
-        return op("v", lambda e: e.tensor_tensor_scan(out, a, b, init, o0, o1), r, w)
+    def scan(out, a, b, init, o0, o1):
+        return op("v", lambda e: e.tensor_tensor_scan(ap(out), ap(a), ap(b), init, o0, o1), [a, b], [out])
 
-    def turn(out, a, r, w):
-        return op("v", lambda e: e.transpose(out, a), r, w)
+    def turn(out, a):
+        return op("v", lambda e: e.transpose(ap(out), ap(a)), [a], [out])
 
-    def fill(ap, val, w):
-        return op("v", lambda e: e.memset(ap, val), (), w)
+    def fill(out, val):
+        return op("v", lambda e: e.memset(ap(out), val), (), [out])
 
-    def quant(q, s, a, r, w):
-        return op("v", lambda e: e.quantize_mx(q, s, a), r, w)
+    def quant(q, s, a, b, src):
+        return op("v", lambda e: e.quantize_mx(ap(V(q, a, b)), ap(V(s, a, b)), ap(src)), [src], [V(q, a, b), V(s, a, b)])
 
-    def act(out, a, func, r, w, **kw):
-        return op("s", lambda e: e.activation(out, a, func, **kw), r, w)
+    def act(out, a, func=F.Copy, **kw):
+        acc = kw.get("accum_out")
+        return op("s", lambda e: e.activation(ap(out), ap(a), func, **{k: ap(x) for k, x in kw.items()}),
+                  [a, kw.get("bias"), kw.get("scale")], [out, acc])
 
-    def mm(b, n, lq, ls, rq, rs, r, start=True, stop=True, ext=()):
-        out = T.ps[:, 512 * b:512 * b + n]
-        return op("t", lambda e: e.matmul_mx(out, lq, ls, rq, rs, start, stop), r, ["@%d" % b], ext=ext)
+    def mm(b, left, a, right, c, n, start=True, stop=True, ext=()):
+        v = [V(left[0], a, a + 128), V(left[1], a, a + 128), V(right[0], c, c + n), V(right[1], c, c + n)]
+        return op("t", lambda e: e.matmul_mx(ap(bank(b, 0, n)), ap(v[0]), ap(v[1]), ap(v[2]), ap(v[3]), start, stop), v,
+                  [bank(b, 0, n)], ext=ext)
 
-    def bank(b, a, n):
-        return T.ps[:, 512 * b + a:512 * b + n]
+    def iota(out, pattern, base, cm=0):
+        if SCRATCH[out[0]][2] == I32:
+            return op("g", lambda e: e.iota(ap(out), pattern, base, cm), (), [out])
+        return op("g", lambda e: e.iota(ap(out), pattern, base, cm, allow_small_or_imprecise_dtypes=True), (), [out])
 
-    def iota(out, pattern, base, cm, w, r=(), small=True):
-        if small:
-            return op("g", lambda e: e.iota(out, pattern, base, cm, allow_small_or_imprecise_dtypes=True), r, w)
-        return op("g", lambda e: e.iota(out, pattern, base, cm), r, w)
-
+    QX, QU, QR, QV, QE, QB, QG, QF, QL, QM, QH = [("q" + x, "s" + x) for x in "xurvebgflmh"]
     sent, lands = [0], []
     for t in range(R):
         src = T.cores[(rank + 1 + t) % N]
@@ -173,290 +215,284 @@ def rank_program(g, core, T, topo):
         sent[0] += 2 * len(topo.engines(core, dst))
         arr = T.sem["arr%d" % t]
         op("g", lambda e: e.remote_dma(T["lq%d" % t][:].bitcast(dt.uint8), T.wq[:].bitcast(dt.uint8), arr, T.sem.sent, pid, rid, mask),
-           ["wq"], (), "remote", after)
-        op("g", lambda e: e.remote_dma(T["lp%d" % t][:], T.wp[:], arr, T.sem.sent, pid, rid, mask), ["wp"], (), "remote")
+           [V("wq")], (), "remote", after)
+        op("g", lambda e: e.remote_dma(T["lp%d" % t][:], T.wp[:], arr, T.sem.sent, pid, rid, mask), [V("wp")], (), "remote")
 
-    PF, QF, GRP, E16, SG, NT, N160, QB, SQ2 = [T.cf[:, i:i + 1] for i in range(9)]
-    XA, XB = ["x0", "x1", "x2", "x3"], ["x0", "x1", "x2", "x4"]
+    PF, Q, GRP, E16, NT, N160, RC, WF, Q256 = [col("cf", i) for i in range(9)]
 
     def tail(h):
-        lo = 16 * (NB - 3 - 4 * h) if h < 4 else 16
-        n = 4 * (TILE_W[h] - lo)
-        return T.ft[:, 4 * (TILE_0[h] + lo):4 * (TILE_0[h] + lo) + n], n, ["f%d" % (4 * h + s) for s in range(4)]
+        return V("ft", 4 * (TILE_0[h + 1] - 48), 4 * TILE_0[h + 1])
 
-    dma("y", T.ut[:], T.u[:], (), ["ut"])
-    dma("y", T.xt[:], T.x[:], (), ["x3", "x4"])
-    dma("s", T.li[:], T.l[:], (), ["li"])
-    dma("s", T.mi[:], T.m[:], (), ["mi"])
-    dma("y", T.wq[:].bitcast(dt.uint8), T.wc[:], (), ["wq"])
-    dma("y", T.wp[:], T.ws[:], (), ["wp"])
-    dma("y", T.vt[:], T.v[:], (), ["vt"])
+    def zero(q, v):
+        n = v[2].stop - v[2].start
+        return act(v, V("zz", 0, n)) if q == "s" else dma(q, v, V("zz", 0, n))
 
-    iota(T.ci[:, 0:1], [[0, 1]], 0, 1, ["ci0"], small=False)
-    iota(T.tm[:], [[0, NB], [1, 16]], 0, 0, ["tm"])
-    iota(T.i1[:], [[1024, 32]], 1024 * 128, -1024, ["i1"], small=False)
-    iota(T.boi[:], [[1, 8], [0, 16]], 0, 0, ["boi"])
-    iota(T.ei[:], [[1, 128]], 0, -1, ["ei"])
-    iota(T.repi[:], [[16, 8]], 0, 0, ["repi"], small=False)
-    iota(T.jj[:], [[1, C]], 0, 0, ["jj"])
-    iota(T.rci[:], [[16, NB]], 15, 0, ["rci"])
-    iota(T.rt[:, 0:16], [[32, 2], [192, 2], [1, 4]], 1, 0, ["rt0"])
-    iota(T.rt[:, 16:32], [[32, 2], [192, 2], [1, 4]], 17, 0, ["rt1"])
-    iota(T.rt[:, 32:64], [[16, 2], [32, 8], [192, 2]], 8, 0, ["rt2"])
-    iota(T.cpat[:], [[64, 4]], 0, 0, ["cpat"])
-    for h in (3, 4):
-        ap, n, tags = tail(h)
-        iota(ap, [[0, n]], 0, 0, tags)
-    iota(T.kci[:], [[16, 8]], 128, 0, ["kci"])
-    iota(T.m4i[:], [[0, 16], [1, 4]], 0, 0, ["m4i"])
-    send(0)
-    iota(T.kv[:], [[1, K]], 1, 0, ["kv"])
-    for c in range(KB):
-        iota(T.eri[:, c:c + 1], [[0, 1]], SEG_0[c + 1] - 1, 0, ["eri%d" % c])
-    iota(T.eri[:, KB:16], [[0, 16 - KB]], 0, 0, ["eri%d" % KB])
-    fill(T.zz[:], 0.0, ["zz"])
-    fill(T.et[:], 0.0, ["et"])
-    fill(NT, -TINY, ["nt"])
-    quant(T.qf[:, 768:896], T.sf[:, 768:896], T.et[:, 0:512], ["et"], ["qfz", "qf3"])
-    fill(N160, -160.0, ["n160"])
-    for h in range(3):
-        ap, n, tags = tail(h)
-        act(ap, T.zz[:, 0:n], F.Copy, ["zz"], tags)
-    act(T.rsb[:], T.zz[:, 0:20], F.Copy, ["zz"], ["rs%d" % c for c in range(NB)])
-    ts(T.ci[:, 1:2], T.ci[:, 0:1], 15, None, A.bitwise_and, None, ["ci0"], ["ci1"])
-    ts(T.ci[:, 2:3], T.ci[:, 0:1], 4, None, A.arith_shift_right, None, ["ci0"], ["ci2"])
-    ts(T.ci[:, 3:4], T.ci[:, 0:1], 16, None, A.bitwise_and, None, ["ci0"], ["ci3"])
-    cp(T.cf[:, 0:4], T.ci[:, 0:4], ["ci0", "ci1", "ci2", "ci3"], ["pf", "qf", "grp"])
-    ts(QB, QF, -BIG, None, A.mult, None, ["qf"], ["qbig"])
-    ts(SQ2, QF, 15.0, 2.0, A.is_equal, A.mult, ["qf"], ["sq2"])
-    ts(T.d0[:], T.tm[:], QF, -BIG, A.is_le, A.mult, ["tm", "qf"], ["d0"])
-    ts(T.i2[:], T.i1[:], 15 * 1024, None, A.bitwise_and, None, ["i1"], ["i2"])
-    act(T.k1[:], T.tm[:], F.Abs, ["tm", "qbig"], ["k1"], bias=QB, scale=BIG)
-    act(T.mne[:], T.k1[:], F.Sign, ["k1"], ["mne"])
-    ts(SG, SQ2, 1.0, None, A.subtract, None, ["sq2"], ["sgc"])
-    ts(T.c16[:, 0:32], T.i2[:], 1025.0, 1.0, A.subtract, A.min, ["i2"], ["c16"])
-    for a, n in ((32, 32), (64, 64), (128, 128), (256, 64)):
-        act(T.c16[:, a:a + n], T.c16[:, 0:n], F.Copy, ["c16"], ["c16"])
-    act(T.win[:], T.zz[:], F.Copy, ["zz"], ["win"])
-    for s in range(4):
-        ts(T.bot[:, s:512:4], T.boi[:], GRP, None, A.is_equal, None, ["boi", "grp"], ["bot%d" % s])
-    ts(T.et[:, 3:515:4], T.ei[:], 0.0, None, A.is_equal, None, ["ei"], ["et"])
-    quant(T.qb[:], T.sb[:], T.bot[:], ["bot%d" % s for s in range(4)], ["qb"])
-    cp(T.repl[:], T.repi[:], ["repi"], ["repl"])
+    dma("y", V("ut"), T.u[:])
+    dma("y", V("xt"), T.x[:])
+    dma("s", V("li"), T.l[:])
+    dma("s", V("mi"), T.m[:])
+    dma("y", as_(V("wq"), dt.uint8), T.wc[:])
+    dma("y", V("wp"), T.ws[:])
+
+    iota(col("ci", 0), [[0, 1]], 0, 1)
+    iota(V("ei"), [[1, 128]], 0, -1)
+    iota(V("tm"), [[0, NB], [1, 16]], 0)
+    iota(V("repi"), [[16, 8]], 0)
+    iota(V("boi"), [[1, 8], [0, 16]], 0)
+    iota(V("jj"), [[1, C]], 0)
+    iota(V("rci"), [[16, NB]], 15 + 15 * int(STEP))
+    fill(V("zz"), 0.0)
+    for h in (2, 3, 4):
+        zero("y", tail(h))
+    for v in (V("win"), V("tl"), V("g0t"), V("tr", 384, 448), V("md", 0, SEG_0[HB]), V("es", SEG_ALL - 256, SEG_ALL),
+              V("wn", 2 * W + K, 3 * W), V("wn", 3 * W + K, 4 * W)):
+        zero("y", v)
+    dma("y", V("vt"), T.v[:])
+    zero("s", V("et"))
+    ts(col("ci", 1), col("ci", 0), 15, A.bitwise_and)
+    ts(col("ci", 2), col("ci", 0), 4, A.arith_shift_right)
+    ts(col("ci", 3), col("ci", 0), 16, A.bitwise_and)
+    fill(NT, -TINY)
+    fill(N160, -160.0)
+    cp(V("cf", 0, 4), V("ci", 0, 4))
+    for a in (960, 1088):
+        quant("qf", "sf", a, a + 128, V("zz", 0, 512))
+    zero("s", tail(0))
+    zero("s", tail(1))
+    ts(V("et", 3, 515, 4), V("ei"), 0.0, A.is_equal, -0.5, A.mult)
+    ts(RC, Q, -STEP - 1.0, A.mult, E16, A.add)
+    ts(V("k1"), V("tm"), Q, A.not_equal, BIG, A.mult)
+    ts(V("d0"), V("tm", 0, H), Q, A.is_le, -BIG, A.mult)
+    cp(V("repl"), V("repi"))
+    act(V("mne"), V("k1"), F.Sign)
+    act(V("c16"), V("mne"), F.Identity, scale=-(STEP + LIFT), bias=LIFT)
     for b in range(4):
-        quant(T.qe[:, 128 * b:128 * b + 128], T.se[:, 128 * b:128 * b + 128], T.et[:, 3 - b:515 - b], ["et"], ["qe%d" % b])
-    fill(T.md[:], 0.0, ["md"])
-    for c in range(1, HB):
-        iota(T.md[:, SEG_0[c]:SEG_0[c] + 1], [[0, 1]], 4, 0, ["me%d" % c], ["md"])
-    cp(T.l16[:], T.li[:], ["li"], ["l16"])
-    cp(T.m16[:], T.mi[:], ["mi"], ["m16"])
-    act(T.lr[:], T.jj[:].indirect(T.l16[:]), F.Identity, ["jj", "l16", "n160"], ["lr"], bias=N160)
-    quant(T.qu[:], T.su[:], T.ut[:], ["ut"], ["qu"])
-    fill(T.g0t[:], 0.0, ["g0t"])
-    cp(T.qr[:].bitcast(dt.uint32), T.qu[:].bitcast(dt.uint32).indirect(T.repl[:]), ["qu", "repl"], ["qr"])
-    act(T.sr[:], T.su[:].indirect(T.repl[:]), F.Copy, ["qu", "repl"], ["sr"])
-    ts(T.rc[:], T.rci[:], QF, E16, A.subtract, A.add, ["rci", "qf", "grp"], ["rc"])
-    fill(T.tl[:], 0.0, ["tl"])
-    act(T.mr[:], T.jj[:].indirect(T.m16[:]), F.Identity, ["jj", "m16", "n160"], ["mr"], bias=N160)
+        quant("qe", "se", 128 * b, 128 * b + 128, V("et", 3 - b, 515 - b))
+        if b == 1:
+            ts(V("bot", 0, 512, 4), V("boi"), GRP, A.is_equal)
+            quant("qu", "su", 0, 128, V("ut"))
+            cp(V("l16"), V("li"))
+            cp(as_(V("qr"), dt.uint32), by(as_(V("qu"), dt.uint32), V("repl")))
+            act(V("bot", 1, 512, 4), V("bot", 0, 512, 4))
+            act(V("sr"), by(V("su"), V("repl")))
+            for s in (2, 3):
+                act(V("bot", s, 512, 4), V("bot", 0, 512, 4))
+    cp(V("m16"), V("mi"))
+    scan_0 = TILE_0[SCAN_FROM]
+    iota(V("rmask", scan_0, 960), [[0, 960 - scan_0]], 1)
+    for h in range(SCAN_FROM, 5):
+        iota(col("rmask", TILE_0[h]), [[0, 1]], 0)
+    send(0)
+    iota(V("rt", 0, 16), [[32, 2], [192, 2], [1, 4]], 1)
+    iota(V("rt", 16, 32), [[32, 2], [192, 2], [1, 4]], 17)
+    iota(V("rt", 32, 64), [[16, 2], [32, 8], [192, 2]], 8)
+    for c in range(HB):
+        iota(V("rt", 64 + c, 96, HB), [[0, 2], [SEG_0[HB], 16 // HB]], SEG_0[c + 1] - 1)
+    iota(V("cpat"), [[64, 4]], 0)
+    iota(V("kci"), [[16, 8]], 128)
+    iota(V("m4"), [[0, 64]], 1)
+    iota(V("m4", 0, 64, 4), [[0, 16]], 0)
+    iota(V("y0", 0, 48, 3), [[0, 16]], 0)
+    iota(V("y0", 2, 48, 3), [[0, 16]], -1)
 
-    def late_constants(part):
-        if part == 0:
-            turn(T.rtt[:], T.rt[:], ["rt0", "rt1", "rt2"], ["rtt"])
-        if part == 1:
-            act(T.tr[:, 384:448], T.zz[:, 0:64], F.Copy, ["zz"], ["trc"])
-            act(T.m4[:], T.m4i[:], F.Sign, ["m4i"], ["m4"])
-            act(T.y0[:], T.zz[:, 0:64], F.Copy, ["zz"], ["y0a", "y0b"])
-            act(T.dh[:, K:4 * DHW:DHW], T.zz[:, 0:4], F.Copy, ["zz"], ["dhz"])
-        if part == 2:
-            ts(T.g1l[:], T.cpat[:], T.rtt[:, 0:1], None, A.add, None, ["cpat", "rtt"], ["g1l"])
-            ts(T.g2l[:], T.jj[:, 0:2], T.rtt[:, 32:33], None, A.add, None, ["jj", "rtt"], ["g2l"])
-        if part == 3:
-            ts(T.g0t[:, 0:512:4], T.tm[:, 0:128], PF, None, A.is_equal, None, ["tm", "pf"], ["g0t"])
-            ts(T.kp[:], T.kci[:], QF, 1.0 / 256, A.add, A.mult, ["kci", "qf"], ["kp"])
-            ts(T.kn[:], T.kci[:], QF, -1.0 / 256, A.add, A.mult, ["kci", "qf"], ["kn"])
-            quant(T.qg[:], T.sg[:], T.g0t[:], ["g0t"], ["qg"])
+    def late(part):
+        if part == "operands":
+            act(V("lr"), by(V("jj"), V("l16")), F.Identity, bias=N160)
+        if part == "ones":
+            quant("qb", "sb", 0, 128, V("bot"))
+            ts(V("rc"), V("rci"), RC, A.add)
+            act(V("mr"), by(V("jj"), V("m16")), F.Identity, bias=N160)
+        if part == "lists":
+            turn(V("rtt"), V("rt"))
+            ts(V("g0t", 0, 512, 4), V("tm", 0, 128), PF, A.is_equal)
+        if part == "lists 2":
+            ts(V("g1l"), V("cpat"), col("rtt", 0), A.add)
+            ts(V("g2l"), V("jj", 0, 2), col("rtt", 32), A.add)
+        if part == "group 0":
+            quant("qg", "sg", 0, 128, V("g0t"))
+        if part == "ends":
+            cp(col("endl", 0), col("rtt", 64))
+            ts(WF, Q, -STEP, A.mult, 15 * STEP, A.add)
+        if part == "firsts":
+            act(Q256, Q, scale=1.0 / 256)
+            act(V("kp"), V("kci"), F.Identity, scale=1.0 / 256, bias=Q256)
+            act(V("kn"), V("kp"), scale=-1.0)
             for c in range(HB):
-                act(T.md[:, SEG_0[c + 1] - 16:SEG_0[c + 1]], T.mne[:, 0:16], F.Identity, ["mne", "kp", "kn", "md"], ["md%d" % c],
-                    bias=T.kn[:, c:c + 1], scale=T.kp[:, c:c + 1])
-        if part == 4:
-            act(T.eri[:, 16:32], T.eri[:, 0:16], F.Copy, ["eri%d" % c for c in range(KB + 1)], ["erj"])
-        if part == 5:
-            turn(T.ert[:], T.eri[:], ["erj"], ["ert"])
-        if part == 6:
-            cp(T.endl[:, 0:1], T.ert[:, 0:1], ["ert"], ["endl"])
-        if part == 7:
-            quant(T.qv[:], T.sv[:], T.vt[:], ["vt"], ["qv"])
+                act(V("md", SEG_0[c + 1] - 17, SEG_0[c + 1] - 1), V("mne", 0, 16), F.Identity, bias=col("kn", c), scale=col("kp", c))
+            for c in range(HB):
+                act(col("md", SEG_0[c + 1] - 1), col("zz", 0), F.Identity, bias=0.25)
+                act(col("md", SEG_0[c]), col("zz", 0), F.Identity, bias=4.0)
+            for h in range(1, PARTS):
+                act(V("md", h * SEG_0[HB], (h + 1) * SEG_0[HB]), V("md", 0, SEG_0[HB]))
 
-    def slot(i, n):
-        h, s = divmod(i, 4)
+    def slot(c, n, name="ft"):
+        h, s = divmod(NB - c, 4)
         a = 4 * TILE_0[h] + s
-        return T.ft[:, a:a + 4 * n - 3:4]
+        return V(name, a, a + 4 * n - 3, 4)
 
-    def qtile(h):
-        a, b, n = CODE_0[h], TILE_0[h], TILE_W[h]
-        quant(T.qf[:, a:a + n], T.sf[:, a:a + n], T.ft[:, 4 * b:4 * (b + n)], ["f%d" % (4 * h + s) for s in range(4)], ["qf%d" % h])
-        if h < 3:
-            n = max(n, 256)
-            mm(3, n - 128, T.qb[:], T.sb[:], T.qf[:, a + 128:a + n], T.sf[:, a + 128:a + n], ["qb", "qf%d" % h, "qfz"], h == 0, h == 2)
-        mm(1, 128, T.qb[:], T.sb[:], T.qf[:, a:a + 128], T.sf[:, a:a + 128], ["qb", "qf%d" % h], h == 0, h == 4)
+    def qtile(h, k):
+        quant("qf", "sf", TILE_0[h], TILE_0[k], V("ft", 4 * TILE_0[h], 4 * TILE_0[k]))
+
+    def sum_tile(h, first=False, last=False):
+        mm(3, QB, 0, QF, TILE_0[h], C if first else TILE_W[h], first, last)
 
     def compare(c):
-        i, n = NB - c, 16 * c
-        ts(slot(i, n), bank(0, 0, n), T.z[:, n + 15:n + 16], None, A.is_lt, None, ["@0", "za", "zb"], ["f%d" % i])
-        if c not in ON_VECTOR:
-            act(T.junk[:, JUNK_0[c]:JUNK_0[c] + n], slot(i, n), F.Identity, ["f%d" % i], ["rs%d" % c, "jk%d" % c],
-                accum_out=T.rsb[:, c:c + 1])
+        n = 16 * c
+        ts(slot(c, n), bank(0, 0, n), col("z", n + 15), A.is_lt)
+        if (NB - c) // 4 < SCAN_FROM:
+            sums.append(c)
 
-    def row_sum(c):
-        n, end = 16 * c, 256 * (c - ON_VECTOR[-1] + 1)
-        scan(T.vj[:, end - n:end], slot(NB - c, n), T.zz[:, 0:n], 0.0, A.add, A.add, ["f%d" % (NB - c), "zz"], ["vj%d" % c])
+    def row_sums(s):
+        scan(V("vj", 4 * scan_0 + 3 - s, 3840, 4), V("rmask", scan_0, 960), V("ft", 4 * scan_0 + s, 3840, 4), 0.0, A.mult, A.add)
 
     def quant_state():
-        quant(T.qx[:, 0:H], T.sx[:, 0:H], T.xt[:, 0:4 * H], XA, ["qx"])
-        quant(T.qx[:, H:C], T.sx[:, H:C], T.xt[:, 4 * H:4 * C], XB, ["qy"])
+        quant("qx", "sx", 0, H, V("xt", 0, 4 * H))
+        quant("qx", "sx", H, C, V("xt", 4 * H, 4 * C))
+
+    def old(b):
+        return V("wn", W * b + K, W * b + W) if b < 2 else V("th", C * (b - 2), C * (b - 1))
 
     for t in range(R):
+        first = late if t == 0 else (lambda part: None)
         quant_state()
-        mm(3, H, T.qr[:], T.sr[:], T.qx[:, 0:H], T.sx[:, 0:H], ["qr", "sr", "qx"])
-        mm(7, H, T.qr[:], T.sr[:], T.qx[:, H:C], T.sx[:, H:C], ["qr", "sr", "qy"])
-        mm(2, C, T.qu[:], T.su[:], T.qx[:], T.sx[:], ["qu", "qx", "qy"])
-        mm(0, C, T.qr[:], T.sr[:], T.qx[:], T.sx[:], ["qr", "sr", "qx", "qy"])
-        mm(1, C, T.qr[:], T.sr[:], T.qx[:], T.sx[:], ["qr", "sr", "qx", "qy"])
-        tt(T.u1[:, 0:H], bank(3, 0, H), T.k1[:, 0:H], A.subtract, ["@3", "k1"], ["u1a"])
-        tt(T.u1[:, H:C], bank(7, 0, H), T.k1[:, H:C], A.subtract, ["@7", "k1"], ["u1b"])
+        mm(3, QR, 0, QX, 0, H)
+        mm(7, QR, 0, QX, H, H)
+        mm(2, QU, 0, QX, 0, C)
+        mm(0, QR, 0, QX, 0, C)
+        mm(1, QR, 0, QX, 0, C)
+        first("operands")
+        tt(V("u1", 0, H), bank(3, 0, H), V("k1", 0, H), A.subtract)
+        tt(V("u1", H, C), bank(7, 0, H), V("k1", 0, H), A.subtract)
         for b in range(4):
-            mm(4 + b, C, T.qe[:, 128 * b:128 * b + 128], T.se[:, 128 * b:128 * b + 128], T.qx[:], T.sx[:], ["qe%d" % b, "qx", "qy"])
-        act(T.bw[:], bank(2, 0, C), F.Sign, ["@2", "nt"], ["bw"], bias=NT)
-        scan(T.z[:, 0:H], T.d0[:, 0:H], T.u1[:, 0:H], 0.0, A.add, A.max, ["d0", "u1a"], ["za"])
-        scan(T.z[:, H:C], T.d0[:, H:C], T.u1[:, H:C], 0.0, A.add, A.max, ["d0", "u1b"], ["zb"])
-        if t == 0:
-            late_constants(0)
+            mm(4 + b, QE, 128 * b, QX, 0, C)
+        act(V("bw"), bank(2, 0, C), F.Sign, bias=NT)
+        scan(V("z", 0, H), V("d0"), V("u1", 0, H), 0.0, A.add, A.max)
+        scan(V("z", H, C), V("d0"), V("u1", H, C), 0.0, A.add, A.max)
+        act(V("gm"), by(V("bw"), V("m16")))
+        first("ones")
         if t == 1:
-            late_constants(7)
-        act(T.gm[:], T.bw[:].indirect(T.m16[:]), F.Copy, ["bw", "m16"], ["gm"])
-        tt(slot(0, C), T.z[:], bank(0, 0, C), A.is_ge, ["za", "zb", "@0"], ["f0"])
+            quant("qv", "sv", 0, 128, V("vt"))
+        iota(V("ww", 0, C), [[1, C]], K)
+        sums = []
         for x in range(len(ON_SCALAR) + 1):
             if x < len(ON_SCALAR):
                 n = 16 * ON_SCALAR[x]
-                act(T.sgn[:, C * x:C * x + n], bank(1, 0, n), F.Sign, ["@1", "za", "zb"], ["sgn%d" % x],
-                    bias=T.z[:, n + 15:n + 16], scale=-1.0)
+                act(V("sgn", C * x, C * x + n), bank(1, 0, n), F.Sign, bias=col("z", n + 15), scale=-1.0)
             if x > 0:
                 c = ON_SCALAR[x - 1]
-                act(slot(NB - c, 16 * c), T.sgn[:, C * (x - 1):C * (x - 1) + 16 * c], F.Relu, ["sgn%d" % (x - 1)],
-                    ["f%d" % (NB - c), "rs%d" % c], accum_out=T.rsb[:, c:c + 1])
-        todo = [c for c in range(NB - 1, 0, -1) if c not in ON_SCALAR]
-        for x, c in enumerate(todo):
+                act(slot(c, 16 * c), V("sgn", C * (x - 1), C * (x - 1) + 16 * c), F.Relu, accum_out=col("rsb", c))
+        tt(slot(NB, C), V("z"), bank(0, 0, C), A.is_ge)
+        todo = [c for c in range(1, NB) if c not in ON_SCALAR]
+        for c in todo:
             compare(c)
-            if x > 0 and todo[x - 1] in ON_VECTOR:
-                row_sum(todo[x - 1])
-            if x > 1 and todo[x - 2] == ON_VECTOR[-1]:
-                lo, n = ON_VECTOR[-1], len(ON_VECTOR)
-                cp(T.rsb[:, lo:lo + n], T.vj[:, 255:256 * n:256], ["vj%d" % y for y in ON_VECTOR], ["rs%d" % y for y in ON_VECTOR])
-            if x == 0:
-                scan(T.dsum[:], T.mne[:], slot(0, C), 0.0, A.mult, A.add, ["mne", "f0"], ["dsum"])
-                tt(T.pp[:], T.bw[:].indirect(T.l16[:]), T.gm[:], A.subtract, ["bw", "l16", "gm"], ["pp", "ppl", "ppm"])
-                pl = dma("y", T.pp[8:128:16, :], T.lr[8:128:16, :], ["lr"], ["ppl"])
-                pm = dma("y", T.pp[9:128:16, :], T.mr[9:128:16, :], ["mr"], ["ppm"])
+            if c == 2:
+                scan(V("dsum"), V("mne"), slot(NB, C), 0.0, A.mult, A.add)
+                tt(V("pp"), by(V("bw"), V("l16")), V("gm"), A.subtract)
+                pl = dma("y", V("pp", parts=slice(8, 128, 16)), V("lr", parts=slice(8, 128, 16)))
+                pm = dma("y", V("pp", parts=slice(9, 128, 16)), V("mr", parts=slice(9, 128, 16)))
                 if t == 0:
                     send(1, [pl, pm])
                     send(2)
-            if x == 1:
-                tt(T.r1[:], T.rc[:], T.dsum[:, 15:C:16], A.subtract, ["rc", "dsum"], ["r1"])
-            for h in QUANT_AFTER.get(c, []):
-                qtile(h)
+            if c == 3:
+                tt(V("r1"), V("rc"), V("dsum", 15, C, 16), A.subtract)
+            if c == 9:
+                qtile(3, 5)
+                sum_tile(4, first=True)
+                sum_tile(3)
+            if c == 13:
+                qtile(2, 3)
+                sum_tile(2)
+        for c in sums:
+            act(slot(c, 16 * c, "junk"), slot(c, 16 * c), F.Identity, accum_out=col("rsb", c))
+        qtile(0, 1)
+        sum_tile(0)
+        row_sums(0)
+        row_sums(1)
+        qtile(1, 2)
+        sum_tile(1, last=True)
+        row_sums(2)
+        row_sums(3)
         for b in range(4):
-            act(T.th[:, C * b:C * b + C], bank(4 + b, 0, C), F.Copy, ["@%d" % (4 + b)], ["th%d" % b], scale=0.5)
-        if t == 0:
-            late_constants(1)
-        for b in range(2):
-            act(T.tt[:, C * b:C * b + C], bank(4 + b, 0, C), F.Copy, ["@%d" % (4 + b)], ["tt%d" % b])
-        act(T.ww[:, 0:C], T.zz[:, 0:C], F.Identity, ["zz"], ["ww"], bias=float(K + 1))
-        tt(T.r2[:], T.r1[:], T.rsb[:], A.subtract, ["r1"] + ["rs%d" % c for c in range(NB)], ["r2"])
-        scan(T.rsc[:, 128:C], T.c16[:, 128:C], bank(3, 0, C - 128), SG, A.mult, A.min, ["c16", "@3", "sgc"], ["rsd"])
-        ts(T.r3[:], T.r2[:], SG, None, A.mult, None, ["r2", "sgc"], ["r3"])
-        scan(T.rsc[:, 0:128], T.c16[:, 0:128], bank(1, 0, 128), SG, A.mult, A.min, ["c16", "@1", "sgc"], ["rsc"])
-        tt(T.r4[:], T.rsc[:, 15:C:16], T.r3[:], A.add, ["rsc", "rsd", "r3"], ["r4"])
-        if t == 0:
-            late_constants(2)
-        ts(T.pos[:], T.r4[:], SG, None, A.mult, None, ["r4", "sgc"], ["pos"])
-        cp(T.win[:].indirect(T.pos[:]), T.pp[:], ["pos", "pp", "ppl", "ppm"], ["win"])
-        if t == 0:
-            late_constants(3)
-        turn(T.tr[:, 0:K], T.win[:, 0:K], ["win"], ["tra"])
-        turn(T.tr[:, K:2 * K], T.win[:, 16:16 + K], ["win"], ["trb"])
-        TR = ["tra", "trb", "trc"]
-        cp(T.tl[:, 0:256:4], T.tr[:].indirect(T.g1l[:]), TR + ["g1l"], ["tl"])
-        quant(T.ql[:], T.sl[:], T.tl[:], ["tl"], ["ql"])
-        mm(0, 128, T.qg[:], T.sg[:], T.ql[:], T.sl[:], ["qg", "ql"])
-        ts(T.y1[:, 1:64:2], T.tr[:].indirect(T.g2l[:]), 160.0, None, A.add, None, TR + ["g2l"], ["y1o"])
-        tt(T.y0[:, 1:32:2], T.y1[:, 33:64:2], T.y1[:, 1:32:2], A.subtract, ["y1o"], ["y0a"])
-        tt(T.prod[:], bank(0, 0, 64), T.tl[:, 0:256:4], A.mult, ["@0", "tl"], ["prod"])
-        tt(T.y0[:, 33:64:2], T.y1[:, 1:32:2], T.y1[:, 33:64:2], A.subtract, ["y1o"], ["y0b"])
-        scan(T.dsc[:], T.m4[:], T.prod[:], 0.0, A.mult, A.add, ["m4", "prod"], ["dsc"])
-        ts(T.y1[:, 0:32:2], T.dsc[:, 3:64:4], 0.0, None, A.is_lt, None, ["dsc"], ["y1e"])
-        ts(T.y1[:, 32:64:2], T.dsc[:, 3:64:4], 0.0, None, A.is_lt, None, ["dsc"], ["y1f"])
-        scan(T.lrf[:], T.y0[:], T.y1[:], 0.0, A.mult, A.add, ["y0a", "y0b", "y1e", "y1f", "y1o"], ["lrf"])
-        cp(T.lr16[:], T.lrf[:, 1:64:2], ["lrf"], ["lr16"])
-        left, right = T.lr16[:, 0:KB], T.lr16[:, 16:16 + KB]
-        cp(T.rowl[:], T.jj[:].indirect(left), ["jj", "lr16"], ["rowl"])
-        for b in range(4):
-            w = T.th[:, C * b:C * b + C]
-            act(T.gr[:, K * b:K * b + K], w.indirect(right), F.Copy, ["th%d" % b, "lr16"], ["gr%d" % b])
-            tt(T.mt[:, b:4 * K:4], w.indirect(left), T.gr[:, K * b:K * b + K], A.subtract, ["th%d" % b, "lr16", "gr%d" % b], ["mt%d" % b])
-        if t == 0:
-            late_constants(4)
-        for c in range(KB):
-            a = K // 2 * (c // HB)
-            act(T.ee[:, SEG_0[c]:SEG_0[c + 1]], T.rowl[:, a:a + SEG_W[c]], F.Abs, ["rowl", "lrf"], ["ee%d" % c],
-                bias=T.lrf[:, 2 * c + 1:2 * c + 2], scale=-1.0)
-        quant(T.qm[:], T.sm[:], T.mt[:], ["mt0", "mt1", "mt2", "mt3"], ["qm"])
-        lq, lp = T["lq%d" % t], T["lp%d" % t]
-        for b in range(4):
-            mm(b, K, lq[:, 128 * b:128 * b + 128], lp[:, 128 * b:128 * b + 128], T.qm[:], T.sm[:], ["qm"],
-               ext=[("arr%d" % t, lands[t])] if b == 0 else ())
-            act(T.ht[:, b:4 * K:4], bank(b, 0, K), F.Copy, ["@%d" % b], ["ht%d" % b], scale=0.03125)
-        if t == 0:
-            late_constants(5)
-        ts(T.nl[:], T.lrf[:, 1:32:2], -1.0 / 1024, None, A.mult, None, ["lrf"], ["nl"])
-        for h in range(2):
-            a, n = SEG_0[HB * h], SEG_0[HB]
-            scan(T.es[:, a:a + n], T.md[:], T.ee[:, a:a + n], 2.0, A.add, A.min,
-                 ["md%d" % c for c in range(HB)] + ["me%d" % c for c in range(1, HB)] + ["ee%d" % c for c in range(HB * h, HB * h + HB)],
-                 ["es%d" % h])
-            if t == 0 and h == 0:
-                late_constants(6)
-        tt(T.of[:], T.es[:].indirect(T.endl[:, 0:1]), T.nl[:], A.min, ["es0", "es1", "endl", "nl"], ["of"])
-        ts(T.o16[:], T.of[:, 0:KB], -1024.0, None, A.mult, None, ["of"], ["o16"])
-        cp(T.ww[:].indirect(T.o16[:, HB:KB]), T.kv[:, K // 2:K], ["o16", "kv"], ["ww"])
-        quant(T.qh[:], T.sh[:], T.ht[:], ["ht0", "ht1", "ht2", "ht3"], ["qh"])
-        for b, bk in enumerate((4, 5, 0, 1)):
-            mm(bk, K, T.qe[:, 128 * b:128 * b + 128], T.se[:, 128 * b:128 * b + 128], T.qh[:], T.sh[:], ["qe%d" % b, "qh"])
-            act(T.dh[:, DHW * b:DHW * b + K], bank(bk, 0, K), F.Copy, ["@%d" % bk], ["dh%d" % b])
-        cp(T.ww[:].indirect(T.o16[:, 0:HB]), T.kv[:, 0:K // 2], ["o16", "kv"], ["ww"])
-        scan(T.wsc[:], T.c16[:], T.ww[:, 0:C], SG, A.mult, A.min, ["c16", "ww", "sgc"], ["wsc"])
-        ts(T.who[:], T.wsc[:, 15:C:16], SG, 1.0, A.mult, A.subtract, ["wsc", "sgc"], ["who"])
+            act(old(b), bank(4 + b, 0, C))
         for b in (2, 3):
-            act(T.g23[:, C * (b - 2):C * (b - 1)], T.dh[:, DHW * b:DHW * b + K + 1].indirect(T.who[:]), F.Copy,
-                ["dh%d" % b, "dhz", "who"], ["g%d" % b])
-        if t == R - 1:
-            act(T.olr[:, 0:K], T.jj[:].indirect(left), F.Copy, ["jj", "lr16"], ["ol0"])
-            act(T.olr[:, K:2 * K], T.jj[:].indirect(right), F.Copy, ["jj", "lr16"], ["ol1"])
-            dma("y", T.ol[:], T.olr[0:128:16, :], ["ol0", "ol1"])
+            act(V("tf", C * (b - 2), C * (b - 1)), bank(4 + b, 0, C), scale=-2.0)
+        first("firsts")
+        for h in range(SCAN_FROM, 5):
+            c = NB - 4 * h - 3
+            tt(V("r1", c, c + 4), V("r1", c, c + 4), V("vj", 4 * TILE_0[h + 1] - 4, 4 * TILE_0[h + 1]), A.subtract)
+        scan(V("rsc"), V("c16"), bank(3, 0, C), 0.0, A.add, A.min)
+        c = NB - 4 * SCAN_FROM + 1
+        tt(V("r1", c, NB), V("r1", c, NB), V("rsb", c, NB), A.subtract)
+        first("lists")
+        tt(V("r4"), V("rsc", 15, C, 16), V("r1"), A.add)
+        first("lists 2")
+        cp(V("pos"), V("r4"))
+        first("group 0")
+        cp(by(V("win"), V("pos")), V("pp"))
+        first("ends")
+        turn(V("tr", 0, K), V("win", 0, K))
+        turn(V("tr", K, 2 * K), V("win", 16, 16 + K))
+        cp(V("tl", 0, 256, 4), by(V("tr"), V("g1l")))
+        ts(V("y1", 1, 96, 3), by(V("tr"), V("g2l")), 160.0, A.add)
+        quant("ql", "sl", 0, 128, V("tl"))
+        mm(0, QG, 0, QL, 0, 128)
+        tt(V("y0", 1, 48, 3), V("y1", 49, 96, 3), V("y1", 1, 48, 3), A.subtract)
+        tt(V("y1", 2, 48, 3), V("y1", 49, 96, 3), V("y1", 1, 48, 3), A.add)
+        tt(V("prod"), bank(0, 0, 64), V("tl", 0, 256, 4), A.mult)
+        scan(V("dsc"), V("m4"), V("prod"), 0.0, A.mult, A.add)
+        ts(V("y1", 0, 48, 3), V("dsc", 3, 64, 4), 0.0, A.is_lt)
+        scan(V("lrf"), V("y0"), V("y1", 0, 48), 0.0, A.mult, A.add)
+        cp(V("lf16"), V("lrf", 1, 48, 3))
+        cp(V("rt16"), V("lrf", 2, 48, 3))
+        left, right = V("lf16", 0, KB), V("rt16", 0, KB)
+        cp(V("rowl", 0, K), by(V("jj"), left))
+        for b in range(3):
+            act(V("gl", K * b, K * b + K), by(old(b), left))
+        ts(V("nl"), V("lrf", 1, 48, 3), 160.0, A.subtract, -1.0 / 1024, A.mult)
+        cp(V("gl", 3 * K, 4 * K), by(old(3), left))
+        cp(by(V("ee"), col("endl", 0)), V("nl"))
+        for c in range(KB):
+            a = 16 * HB * (c // HB)
+            act(V("ee", SEG_0[c], SEG_0[c + 1] - 1), V("rowl", a, a + SEG_W[c]), F.Abs, bias=col("lrf", 3 * c + 1), scale=-1.0)
+        for b in range(4):
+            tt(V("mt", b, 4 * K, 4), by(old(b), right), V("gl", K * b, K * b + K), A.subtract)
+        quant("qm", "sm", 0, K, V("mt"))
+        for b in range(4):
+            mm(b, ("lq%d" % t, "lp%d" % t), 128 * b, QM, 0, K, ext=[("arr%d" % t, lands[t])] if b == 0 else ())
+            act(V("ht", b, 4 * K, 4), bank(b, 0, K), scale=0.03125)
+        scan(V("es", 0, SEG_0[KB]), V("md"), V("ee", 0, SEG_0[KB]), 2.0, A.add, A.min)
+        ts(V("o16"), by(V("es"), col("endl", 0)), -1024.0, A.mult, 160.0, A.add)
+        for h in range(PARTS - 1, -1, -1):
+            cp(by(V("ww"), V("o16", HB * h, HB * h + HB)), V("jj", 16 * HB * h, 16 * HB * (h + 1)))
+            if h == 1:
+                quant("qh", "sh", 0, K, V("ht"))
+        for b in range(4):
+            mm(4 + b, QE, 128 * b, QH, 0, K)
+        for b in (2, 3):
+            act(V("wn", W * b, W * b + K), bank(4 + b, 0, K), scale=-2.0)
+
+        def new(b):
+            tt(V("wn", W * b, W * b + K), bank(4 + b, 0, K), V("gl", K * b, K * b + K), A.add)
+
+        scan(V("wsc"), V("c16"), V("ww", 0, C), 0.0, A.add, A.min)
+        new(0)
+        ts(V("who"), V("wsc", 15, C, 16), WF, A.add)
+        new(1)
         for b in (0, 1):
-            tt(T.xt[:, b:4 * C:4], T.dh[:, DHW * b:DHW * b + K + 1].indirect(T.who[:]), T.tt[:, C * b:C * b + C], A.add,
-               ["dh%d" % b, "dhz", "who", "tt%d" % b], ["x%d" % b])
-        tt(T.xt[:, 2:4 * C:4], bank(6, 0, C), T.g23[:, 0:C], A.add, ["@6", "g2"], ["x2"])
-        tt(T.xt[:, 3:4 * H:4], bank(7, 0, H), T.g23[:, C:C + H], A.add, ["@7", "g3"], ["x3"])
-        tt(T.xt[:, 4 * H + 3:4 * C:4], bank(7, H, C), T.g23[:, C + H:2 * C], A.add, ["@7", "g3"], ["x4"])
+            act(V("xt", b, 4 * C, 4), by(V("wn", W * b, W * b + W), V("who")), scale=-2.0)
+        for b in (2, 3):
+            tt(V("xt", b, 4 * C, 4), by(V("wn", W * b, W * b + W), V("who")), V("tf", C * (b - 2), C * (b - 1)), A.add)
 
     quant_state()
-    mm(0, H, T.qv[:], T.sv[:], T.qx[:, 0:H], T.sx[:, 0:H], ["qv", "qx"])
-    mm(1, H, T.qv[:], T.sv[:], T.qx[:, H:C], T.sx[:, H:C], ["qv", "qy"])
-    dma("y", T.oc[:], T.qx[:].bitcast(dt.uint8), ["qx", "qy"])
-    act(T.ysb[:, 0:H], bank(0, 0, H), F.Copy, ["@0"], ["ya"])
-    cp(T.ysb[:, H:C], bank(1, 0, H), ["@1"], ["yb"])
+    act(V("rowl", K, 2 * K), by(V("jj"), right))
+    mm(0, QV, 0, QX, 0, H)
+    mm(1, QV, 0, QX, H, H)
+    dma("y", T.oc[:], as_(V("qx"), dt.uint8))
+    act(V("ysb", 0, H), bank(0, 0, H))
+    cp(V("ysb", H, C), bank(1, 0, H))
+    dma("s", T.y[:], V("ysb"))
+    dma("y", T.ol[:], V("rowl", parts=slice(0, 128, 16)))
     for k in range(4):
-        dma("y", T.osc[4 * k:4 * k + 4, :], T.sx[32 * k:32 * k + 4, :], ["qx", "qy"])
-    dma("s", T.y[:], T.ysb[:], ["ya", "yb"])
+        dma("y", T.osc[4 * k:4 * k + 4, :], V("sx", parts=slice(32 * k, 32 * k + 4)))
     plan(g, T, ops)
     g.wait_ge(T.sem.sent, sent[0])

@@ -17,8 +17,8 @@ SEG_W = [16 * (c % HB + 1) for c in range(KB)]
 SEG_0 = [sum(SEG_W[:c]) + c for c in range(KB + 1)]
 SEG_ALL = SEG_0[HB] * 16 // HB
 ON_SCALAR = (19, 18, 17, 16, 15)
-SCAN_FROM = 3
-STEP, LIFT = 512.0, 16384.0
+SUM_V = 9
+STEP, LIFT = 512, 16384
 W = K + C
 
 BF, F32, I32, U16, U8, X4 = "bfloat16", "float32", "int32", "uint16", "uint8", "float8_e4m3fn_x4"
@@ -30,26 +30,26 @@ for _n, _w, _d in [
         ("li", 20, I32), ("mi", 20, I32), ("l16", 20, U16), ("m16", 20, U16),
         ("wq", 512, X4), ("wp", 512, U8), ("lq0", 512, X4), ("lp0", 512, U8), ("lq1", 512, X4), ("lp1", 512, U8),
         ("lq2", 512, X4), ("lp2", 512, U8),
-        ("ci", 8, I32), ("cf", 16, F32), ("tm", 320, BF), ("jj", 320, F32), ("boi", 128, BF),
-        ("ei", 128, BF), ("k1", 320, BF), ("d0", 160, BF), ("mne", 320, BF), ("c16", 320, BF),
+        ("ra", 32, F32), ("rat", 32, F32), ("cf", 8, F32), ("tm", 176, BF), ("jj", 320, F32), ("boi", 128, BF), ("e16", 16, BF),
+        ("k1", 176, BF), ("d0", 160, BF), ("m0", 320, BF), ("c16", 320, BF), ("pr", 320, F32),
         ("zz", 520, BF), ("et", 520, BF), ("qe", 512, X4), ("se", 512, U8), ("bot", 512, BF), ("qb", 128, X4), ("sb", 128, U8),
         ("g0t", 512, BF), ("qg", 128, X4), ("sg", 128, U8),
         ("u1", 320, F32), ("z", 320, F32), ("ft", 3840, BF), ("qf", 1216, X4), ("sf", 1216, U8),
-        ("dsum", 320, BF), ("sgn", 2240, BF), ("vj", 3840, BF), ("junk", 3840, BF), ("rmask", 960, BF),
-        ("rsb", 20, F32), ("rc", 20, F32), ("r1", 20, F32), ("rsc", 320, F32), ("r4", 20, F32), ("pos", 20, U16),
+        ("dsum", 320, BF), ("sgn", C * len(ON_SCALAR), BF), ("vj", 2048, BF), ("junk", 3840, BF),
+        ("rsb", 20, F32), ("rc", 20, F32), ("r1", 20, F32), ("rsc", 320, F32), ("pos", 20, U16),
         ("bw", 320, BF), ("gm", 320, BF), ("pp", 320, BF), ("lr", 320, BF), ("mr", 320, BF), ("win", 336, BF), ("tr", 448, BF),
         ("tl", 512, BF), ("ql", 128, X4), ("sl", 128, U8), ("prod", 64, BF), ("dsc", 64, BF), ("m4", 64, BF),
         ("y0", 48, F32), ("y1", 96, F32), ("lrf", 48, F32), ("lf16", 16, U16), ("rt16", 16, U16),
         ("wn", 4 * W, BF), ("gl", 768, BF), ("mt", 768, BF), ("qm", 192, X4), ("sm", 192, U8),
         ("ht", 768, BF), ("qh", 192, X4), ("sh", 192, U8),
-        ("rowl", 384, F32), ("ee", SEG_ALL, BF), ("md", SEG_0[KB], BF), ("kci", 8, F32), ("kp", 8, F32), ("kn", 8, F32),
-        ("es", SEG_ALL, BF), ("nl", 16, BF), ("th", 640, BF), ("tf", 640, BF), ("o16", 16, U16), ("ww", 896, F32),
+        ("olr", 384, F32), ("ee", SEG_ALL, BF), ("md", SEG_0[KB], BF), ("kci", 8, F32), ("kp", 8, F32), ("kn", 8, F32),
+        ("es", SEG_ALL, BF), ("nl", 16, BF), ("th", 640, BF), ("tf", 640, BF), ("o16", 32, U16), ("ww", 896, F32),
         ("wsc", 320, F32), ("who", 20, U16), ("rci", 20, F32),
         ("g1l", 4, U16), ("g2l", 2, U16), ("endl", 2, U16), ("repi", 8, I32), ("repl", 8, U16), ("cpat", 4, F32),
-        ("rt", 96, F32), ("rtt", 96, F32), ("ysb", 320, F32)]:
+        ("rt", 160, F32), ("rtt", 160, F32), ("ysb", 320, F32)]:
     SCRATCH[_n] = ("sbuf", [128, _w], _d)
 
-NDMA = 40
+NDMA = 48
 SEMAPHORES = ["cv", "cs", "ct", "cg", "arr0", "arr1", "arr2", "sent"] + ["d%d" % i for i in range(NDMA)]
 ENGINE_SEM = {"v": "cv", "s": "cs", "t": "ct", "g": "cg"}
 ALL = slice(0, 128)
@@ -218,107 +218,113 @@ def rank_program(g, core, T, topo):
            [V("wq")], (), "remote", after)
         op("g", lambda e: e.remote_dma(T["lp%d" % t][:], T.wp[:], arr, T.sem.sent, pid, rid, mask), [V("wp")], (), "remote")
 
-    PF, Q, GRP, E16, NT, N160, RC, WF, Q256 = [col("cf", i) for i in range(9)]
+    Q, FIX, WF = col("rat", 0), col("rtt", 96), col("rtt", 128)
+    PF, Q256, KEEP, NT = [col("cf", i) for i in range(4)]
 
     def tail(h):
         return V("ft", 4 * (TILE_0[h + 1] - 48), 4 * TILE_0[h + 1])
 
     def zero(q, v):
         n = v[2].stop - v[2].start
+        if q == "g":
+            return iota(v, [[0, n]], 0)
         return act(v, V("zz", 0, n)) if q == "s" else dma(q, v, V("zz", 0, n))
+
+    def lane(name, q):
+        return V(name, parts=slice(q, 128, 16))
 
     dma("y", V("ut"), T.u[:])
     dma("y", V("xt"), T.x[:])
     dma("s", V("li"), T.l[:])
     dma("s", V("mi"), T.m[:])
+
+    def pattern(name):
+        for h in range(2):
+            act(V(name, H * h, H * h + H), V("k1", 1, H + 1), F.Identity, scale=-(STEP + LIFT) / BIG, bias=float(LIFT))
+
+    iota(V("ra"), [[0, 2], [1, 16]], 0)
+    iota(V("repi"), [[16, 8]], 0)
+    iota(V("tm"), [[0, 11], [1, 16]], 0)
+    fill(V("zz"), 0.0)
+    iota(PF, [[0, 1]], 0, 1)
+    iota(V("jj"), [[1, C]], 0)
+    iota(V("boi"), [[16, 8], [0, 16]], 0, -1)
+    iota(V("rci"), [[16, NB]], 15)
+    iota(V("rsb"), [[0, NB]], 0)
+    for h in (4, 3):
+        zero("s", tail(h))
+    for v in (tail(0), tail(2), tail(1), V("et")):
+        zero("y", v)
     dma("y", as_(V("wq"), dt.uint8), T.wc[:])
     dma("y", V("wp"), T.ws[:])
-
-    iota(col("ci", 0), [[0, 1]], 0, 1)
-    iota(V("ei"), [[1, 128]], 0, -1)
-    iota(V("tm"), [[0, NB], [1, 16]], 0)
-    iota(V("repi"), [[16, 8]], 0)
-    iota(V("boi"), [[1, 8], [0, 16]], 0)
-    iota(V("jj"), [[1, C]], 0)
-    iota(V("rci"), [[16, NB]], 15 + 15 * int(STEP))
-    fill(V("zz"), 0.0)
-    for h in (2, 3, 4):
-        zero("y", tail(h))
-    for v in (V("win"), V("tl"), V("g0t"), V("tr", 384, 448), V("md", 0, SEG_0[HB]), V("es", SEG_ALL - 256, SEG_ALL),
-              V("wn", 2 * W + K, 3 * W), V("wn", 3 * W + K, 4 * W)):
-        zero("y", v)
+    zero("y", V("g0t"))
     dma("y", V("vt"), T.v[:])
-    zero("s", V("et"))
-    ts(col("ci", 1), col("ci", 0), 15, A.bitwise_and)
-    ts(col("ci", 2), col("ci", 0), 4, A.arith_shift_right)
-    ts(col("ci", 3), col("ci", 0), 16, A.bitwise_and)
-    fill(NT, -TINY)
-    fill(N160, -160.0)
-    cp(V("cf", 0, 4), V("ci", 0, 4))
+    turn(V("rat"), V("ra"))
     for a in (960, 1088):
         quant("qf", "sf", a, a + 128, V("zz", 0, 512))
-    zero("s", tail(0))
-    zero("s", tail(1))
-    ts(V("et", 3, 515, 4), V("ei"), 0.0, A.is_equal, -0.5, A.mult)
-    ts(RC, Q, -STEP - 1.0, A.mult, E16, A.add)
-    ts(V("k1"), V("tm"), Q, A.not_equal, BIG, A.mult)
-    ts(V("d0"), V("tm", 0, H), Q, A.is_le, -BIG, A.mult)
     cp(V("repl"), V("repi"))
-    act(V("mne"), V("k1"), F.Sign)
-    act(V("c16"), V("mne"), F.Identity, scale=-(STEP + LIFT), bias=LIFT)
-    for b in range(4):
-        quant("qe", "se", 128 * b, 128 * b + 128, V("et", 3 - b, 515 - b))
-        if b == 1:
-            ts(V("bot", 0, 512, 4), V("boi"), GRP, A.is_equal)
-            quant("qu", "su", 0, 128, V("ut"))
-            cp(V("l16"), V("li"))
-            cp(as_(V("qr"), dt.uint32), by(as_(V("qu"), dt.uint32), V("repl")))
-            act(V("bot", 1, 512, 4), V("bot", 0, 512, 4))
-            act(V("sr"), by(V("su"), V("repl")))
-            for s in (2, 3):
-                act(V("bot", s, 512, 4), V("bot", 0, 512, 4))
+    ts(KEEP, Q, 14.0, A.is_lt)
+    ts(NT, Q, 14.0, A.is_lt, -TINY, A.mult)
+    for h in range(2):
+        act(V("m0", H * h, H * h + H), V("tm", 0, H), F.Sign)
+    ts(V("k1"), V("tm"), Q, A.not_equal, BIG, A.mult)
+    pattern("pr")
+    ts(V("d0"), V("tm", 0, H), 0.0, A.is_equal, -BIG, A.mult)
+    cp(V("l16"), V("li"))
+    quant("qu", "su", 0, 128, V("ut"))
     cp(V("m16"), V("mi"))
-    scan_0 = TILE_0[SCAN_FROM]
-    iota(V("rmask", scan_0, 960), [[0, 960 - scan_0]], 1)
-    for h in range(SCAN_FROM, 5):
-        iota(col("rmask", TILE_0[h]), [[0, 1]], 0)
-    send(0)
+    cp(as_(V("qr"), dt.uint32), by(as_(V("qu"), dt.uint32), V("repl")))
+    act(V("sr"), by(V("su"), V("repl")))
+    act(V("lr"), by(V("jj"), V("l16")), F.Identity, bias=160.0, scale=-1.0)
+    act(V("mr"), by(V("jj"), V("m16")), F.Identity, bias=160.0, scale=-1.0)
+    iota(V("rt", 96, 128), [[16, 2], [-STEP - 1, 16]], 16 * STEP)
+    iota(V("rt", 128, 160), [[0, 2], [-STEP, 16]], 16 * STEP)
     iota(V("rt", 0, 16), [[32, 2], [192, 2], [1, 4]], 1)
     iota(V("rt", 16, 32), [[32, 2], [192, 2], [1, 4]], 17)
-    iota(V("rt", 32, 64), [[16, 2], [32, 8], [192, 2]], 8)
+    iota(V("rt", 32, 64), [[16, 2], [32, 8], [192, 2]], 14)
+    iota(V("rt", 96, 128, 16), [[16, 2]], 15 * STEP - LIFT)
+    iota(V("rt", 128, 160, 16), [[0, 2]], 15 * STEP - LIFT)
     for c in range(HB):
         iota(V("rt", 64 + c, 96, HB), [[0, 2], [SEG_0[HB], 16 // HB]], SEG_0[c + 1] - 1)
     iota(V("cpat"), [[64, 4]], 0)
     iota(V("kci"), [[16, 8]], 128)
     iota(V("m4"), [[0, 64]], 1)
-    iota(V("m4", 0, 64, 4), [[0, 16]], 0)
     iota(V("y0", 0, 48, 3), [[0, 16]], 0)
+    iota(V("m4", 0, 64, 4), [[0, 16]], 0)
     iota(V("y0", 2, 48, 3), [[0, 16]], -1)
+    for v in (V("win"), V("md", 0, SEG_0[HB]), V("tr", 384, 448)):
+        zero("g", v)
 
     def late(part):
-        if part == "operands":
-            act(V("lr"), by(V("jj"), V("l16")), F.Identity, bias=N160)
+        if part == "block ones":
+            for s in range(4):
+                ts(V("bot", s, 512, 4), V("boi"), Q, A.add, 0.0, A.is_equal)
+            ts(V("rc"), V("rci"), col("pr", 15), A.add)
+        if part == "identity":
+            ts(V("et", 3, 515, 4), V("jj", 0, 128), PF, A.is_equal, -0.5, A.mult)
         if part == "ones":
             quant("qb", "sb", 0, 128, V("bot"))
-            ts(V("rc"), V("rci"), RC, A.add)
-            act(V("mr"), by(V("jj"), V("m16")), F.Identity, bias=N160)
         if part == "lists":
             turn(V("rtt"), V("rt"))
+        if part in range(4):
+            quant("qe", "se", 128 * part, 128 * part + 128, V("et", 3 - part, 515 - part))
+            unpack(part)
+        if part == "signs":
             ts(V("g0t", 0, 512, 4), V("tm", 0, 128), PF, A.is_equal)
-        if part == "lists 2":
             ts(V("g1l"), V("cpat"), col("rtt", 0), A.add)
-            ts(V("g2l"), V("jj", 0, 2), col("rtt", 32), A.add)
         if part == "group 0":
             quant("qg", "sg", 0, 128, V("g0t"))
+            ts(V("g2l"), V("jj", 0, 2), col("rtt", 32), A.add)
         if part == "ends":
             cp(col("endl", 0), col("rtt", 64))
-            ts(WF, Q, -STEP, A.mult, 15 * STEP, A.add)
         if part == "firsts":
+            pattern("c16")
+            act(V("e16"), V("k1", 0, 16), F.Sign)
             act(Q256, Q, scale=1.0 / 256)
             act(V("kp"), V("kci"), F.Identity, scale=1.0 / 256, bias=Q256)
             act(V("kn"), V("kp"), scale=-1.0)
             for c in range(HB):
-                act(V("md", SEG_0[c + 1] - 17, SEG_0[c + 1] - 1), V("mne", 0, 16), F.Identity, bias=col("kn", c), scale=col("kp", c))
+                act(V("md", SEG_0[c + 1] - 17, SEG_0[c + 1] - 1), V("e16"), F.Identity, bias=col("kn", c), scale=col("kp", c))
             for c in range(HB):
                 act(col("md", SEG_0[c + 1] - 1), col("zz", 0), F.Identity, bias=0.25)
                 act(col("md", SEG_0[c]), col("zz", 0), F.Identity, bias=4.0)
@@ -336,44 +342,49 @@ def rank_program(g, core, T, topo):
     def sum_tile(h, first=False, last=False):
         mm(3, QB, 0, QF, TILE_0[h], C if first else TILE_W[h], first, last)
 
-    def compare(c):
-        n = 16 * c
-        ts(slot(c, n), bank(0, 0, n), col("z", n + 15), A.is_lt)
-        if (NB - c) // 4 < SCAN_FROM:
-            sums.append(c)
+    def row_sum(c):
+        n, a = 8 * c, slot(c, 16 * c)[2].start
+        scan(V("vj", 16 * (128 - n) + c, 2048, 16), V("ft", a, a + 4 * n - 3, 4), V("ft", a + 4 * n, a + 8 * n - 3, 4), 0.0, A.add, A.add)
 
-    def row_sums(s):
-        scan(V("vj", 4 * scan_0 + 3 - s, 3840, 4), V("rmask", scan_0, 960), V("ft", 4 * scan_0 + s, 3840, 4), 0.0, A.mult, A.add)
+    def quant_half(h):
+        quant("qx", "sx", H * h, H * (h + 1), V("xt", 4 * H * h, 4 * H * (h + 1)))
 
-    def quant_state():
-        quant("qx", "sx", 0, H, V("xt", 0, 4 * H))
-        quant("qx", "sx", H, C, V("xt", 4 * H, 4 * C))
+    def unpack(b):
+        mm(4 + b, QE, 128 * b, QX, 0, C)
 
     def old(b):
         return V("wn", W * b + K, W * b + W) if b < 2 else V("th", C * (b - 2), C * (b - 1))
 
+    def pack(name, b):
+        return V(name, K * b, K * b + K)
+
     for t in range(R):
         first = late if t == 0 else (lambda part: None)
-        quant_state()
+        quant_half(0)
+        quant_half(1)
         mm(3, QR, 0, QX, 0, H)
         mm(7, QR, 0, QX, H, H)
         mm(2, QU, 0, QX, 0, C)
         mm(0, QR, 0, QX, 0, C)
         mm(1, QR, 0, QX, 0, C)
-        first("operands")
+        first("block ones")
         tt(V("u1", 0, H), bank(3, 0, H), V("k1", 0, H), A.subtract)
         tt(V("u1", H, C), bank(7, 0, H), V("k1", 0, H), A.subtract)
-        for b in range(4):
-            mm(4 + b, QE, 128 * b, QX, 0, C)
-        act(V("bw"), bank(2, 0, C), F.Sign, bias=NT)
+        for b in range(4 if t > 0 else 0):
+            unpack(b)
+        act(V("bw"), bank(2, 0, C), F.Sign, bias=NT, scale=KEEP)
         scan(V("z", 0, H), V("d0"), V("u1", 0, H), 0.0, A.add, A.max)
         scan(V("z", H, C), V("d0"), V("u1", H, C), 0.0, A.add, A.max)
         act(V("gm"), by(V("bw"), V("m16")))
-        first("ones")
-        if t == 1:
-            quant("qv", "sv", 0, 128, V("vt"))
+        rows = [dma("y", lane("gm", 14), lane("lr", 14)), dma("y", lane("gm", 15), lane("mr", 15))]
+        if t == 0:
+            send(0, rows)
+            for v in (V("tl"), V("es"), V("wn", 2 * W + K, 3 * W), V("wn", 3 * W + K, 4 * W)):
+                zero("g", v)
         iota(V("ww", 0, C), [[1, C]], K)
-        sums = []
+        if t == 0:
+            send(1)
+            send(2)
         for x in range(len(ON_SCALAR) + 1):
             if x < len(ON_SCALAR):
                 n = 16 * ON_SCALAR[x]
@@ -381,63 +392,62 @@ def rank_program(g, core, T, topo):
             if x > 0:
                 c = ON_SCALAR[x - 1]
                 act(slot(c, 16 * c), V("sgn", C * (x - 1), C * (x - 1) + 16 * c), F.Relu, accum_out=col("rsb", c))
-        tt(slot(NB, C), V("z"), bank(0, 0, C), A.is_ge)
-        todo = [c for c in range(1, NB) if c not in ON_SCALAR]
-        for c in todo:
-            compare(c)
+        for c in range(1, ON_SCALAR[-1]):
+            ts(slot(c, 16 * c), bank(0, 0, 16 * c), col("z", 16 * c + 15), A.is_lt)
             if c == 2:
-                scan(V("dsum"), V("mne"), slot(NB, C), 0.0, A.mult, A.add)
-                tt(V("pp"), by(V("bw"), V("l16")), V("gm"), A.subtract)
-                pl = dma("y", V("pp", parts=slice(8, 128, 16)), V("lr", parts=slice(8, 128, 16)))
-                pm = dma("y", V("pp", parts=slice(9, 128, 16)), V("mr", parts=slice(9, 128, 16)))
-                if t == 0:
-                    send(1, [pl, pm])
-                    send(2)
-            if c == 3:
+                tt(slot(NB, C), V("z"), bank(0, 0, C), A.is_ge)
+            if c == 4:
+                scan(V("dsum"), V("m0"), slot(NB, C), 0.0, A.mult, A.add)
+                first("identity")
+            if c == 5:
                 tt(V("r1"), V("rc"), V("dsum", 15, C, 16), A.subtract)
             if c == 9:
+                first("ones")
                 qtile(3, 5)
                 sum_tile(4, first=True)
                 sum_tile(3)
-            if c == 13:
-                qtile(2, 3)
-                sum_tile(2)
-        for c in sums:
+        for c in range(1, SUM_V):
             act(slot(c, 16 * c, "junk"), slot(c, 16 * c), F.Identity, accum_out=col("rsb", c))
+        row_sum(SUM_V)
+        qtile(2, 3)
+        sum_tile(2)
+        row_sum(SUM_V + 1)
         qtile(0, 1)
         sum_tile(0)
-        row_sums(0)
-        row_sums(1)
+        for c in range(SUM_V + 2, ON_SCALAR[-1]):
+            row_sum(c)
         qtile(1, 2)
         sum_tile(1, last=True)
-        row_sums(2)
-        row_sums(3)
-        for b in range(4):
+        mine = V("r1", SUM_V, ON_SCALAR[-1])
+        tt(mine, mine, V("vj", 2032 + SUM_V, 2032 + ON_SCALAR[-1]), A.subtract)
+        tt(V("pp"), by(V("bw"), V("l16")), V("gm"), A.subtract)
+        tt(V("pr", 15, C, 16), V("r1"), V("rsb"), A.subtract)
+        first("lists")
+        scan(V("rsc"), bank(3, 0, C), V("pr"), float(LIFT), A.min, A.add)
+        first(2)
+        ts(V("pos"), V("rsc", 15, C, 16), FIX, A.add)
+        first(3)
+        cp(by(V("win"), V("pos")), V("pp"))
+        first(0)
+        turn(V("tr", 0, K), V("win", 0, K))
+        first("signs")
+        turn(V("tr", K, 2 * K), V("win", 16, 16 + K))
+        first(1)
+        first("firsts")
+        for b in (2, 3, 0, 1):
             act(old(b), bank(4 + b, 0, C))
         for b in (2, 3):
             act(V("tf", C * (b - 2), C * (b - 1)), bank(4 + b, 0, C), scale=-2.0)
-        first("firsts")
-        for h in range(SCAN_FROM, 5):
-            c = NB - 4 * h - 3
-            tt(V("r1", c, c + 4), V("r1", c, c + 4), V("vj", 4 * TILE_0[h + 1] - 4, 4 * TILE_0[h + 1]), A.subtract)
-        scan(V("rsc"), V("c16"), bank(3, 0, C), 0.0, A.add, A.min)
-        c = NB - 4 * SCAN_FROM + 1
-        tt(V("r1", c, NB), V("r1", c, NB), V("rsb", c, NB), A.subtract)
-        first("lists")
-        tt(V("r4"), V("rsc", 15, C, 16), V("r1"), A.add)
-        first("lists 2")
-        cp(V("pos"), V("r4"))
-        first("group 0")
-        cp(by(V("win"), V("pos")), V("pp"))
-        first("ends")
-        turn(V("tr", 0, K), V("win", 0, K))
-        turn(V("tr", K, 2 * K), V("win", 16, 16 + K))
         cp(V("tl", 0, 256, 4), by(V("tr"), V("g1l")))
-        ts(V("y1", 1, 96, 3), by(V("tr"), V("g2l")), 160.0, A.add)
+        first("group 0")
         quant("ql", "sl", 0, 128, V("tl"))
+        ts(V("y1", 1, 96, 3), by(V("tr"), V("g2l")), 160.0, A.add)
         mm(0, QG, 0, QL, 0, 128)
+        first("ends")
         tt(V("y0", 1, 48, 3), V("y1", 49, 96, 3), V("y1", 1, 48, 3), A.subtract)
         tt(V("y1", 2, 48, 3), V("y1", 49, 96, 3), V("y1", 1, 48, 3), A.add)
+        if t == 1:
+            quant("qv", "sv", 0, 128, V("vt"))
         tt(V("prod"), bank(0, 0, 64), V("tl", 0, 256, 4), A.mult)
         scan(V("dsc"), V("m4"), V("prod"), 0.0, A.mult, A.add)
         ts(V("y1", 0, 48, 3), V("dsc", 3, 64, 4), 0.0, A.is_lt)
@@ -445,36 +455,53 @@ def rank_program(g, core, T, topo):
         cp(V("lf16"), V("lrf", 1, 48, 3))
         cp(V("rt16"), V("lrf", 2, 48, 3))
         left, right = V("lf16", 0, KB), V("rt16", 0, KB)
-        cp(V("rowl", 0, K), by(V("jj"), left))
         for b in range(3):
-            act(V("gl", K * b, K * b + K), by(old(b), left))
+            act(pack("gl", b), by(old(b), left))
         ts(V("nl"), V("lrf", 1, 48, 3), 160.0, A.subtract, -1.0 / 1024, A.mult)
-        cp(V("gl", 3 * K, 4 * K), by(old(3), left))
+        cp(pack("gl", 3), by(old(3), left))
         cp(by(V("ee"), col("endl", 0)), V("nl"))
-        for c in range(KB):
-            a = 16 * HB * (c // HB)
-            act(V("ee", SEG_0[c], SEG_0[c + 1] - 1), V("rowl", a, a + SEG_W[c]), F.Abs, bias=col("lrf", 3 * c + 1), scale=-1.0)
-        for b in range(4):
-            tt(V("mt", b, 4 * K, 4), by(old(b), right), V("gl", K * b, K * b + K), A.subtract)
+        for h in range(PARTS - 1, -1, -1):
+            for c in range(HB * h, HB * h + HB):
+                act(V("ee", SEG_0[c], SEG_0[c + 1] - 1), by(V("jj"), V("lf16", HB * h, c + 1)), F.Abs, bias=col("lrf", 3 * c + 1), scale=-1.0)
+        for b in (3, 0, 1, 2):
+            tt(V("mt", b, 4 * K, 4), by(old(b), right), pack("gl", b), A.subtract)
         quant("qm", "sm", 0, K, V("mt"))
         for b in range(4):
             mm(b, ("lq%d" % t, "lp%d" % t), 128 * b, QM, 0, K, ext=[("arr%d" % t, lands[t])] if b == 0 else ())
-            act(V("ht", b, 4 * K, 4), bank(b, 0, K), scale=0.03125)
-        scan(V("es", 0, SEG_0[KB]), V("md"), V("ee", 0, SEG_0[KB]), 2.0, A.add, A.min)
-        ts(V("o16"), by(V("es"), col("endl", 0)), -1024.0, A.mult, 160.0, A.add)
-        for h in range(PARTS - 1, -1, -1):
-            cp(by(V("ww"), V("o16", HB * h, HB * h + HB)), V("jj", 16 * HB * h, 16 * HB * (h + 1)))
-            if h == 1:
-                quant("qh", "sh", 0, K, V("ht"))
-        for b in range(4):
-            mm(4 + b, QE, 128 * b, QH, 0, K)
-        for b in (2, 3):
-            act(V("wn", W * b, W * b + K), bank(4 + b, 0, K), scale=-2.0)
+
+        def firsts(h0, h1):
+            a, b = SEG_0[HB * h0], SEG_0[HB * h1]
+            scan(V("es", a, b), V("md", a, b), V("ee", a, b), 2.0, A.add, A.min)
+
+        def places(x):
+            ts(V("o16", 16 * x, 16 * x + 16), by(V("es"), col("endl", 0)), -1024.0, A.mult, 160.0, A.add)
+
+        def put(h, x):
+            cp(by(V("ww"), V("o16", 16 * x + HB * h, 16 * x + HB * h + HB)), V("jj", 16 * HB * h, 16 * HB * (h + 1)))
 
         def new(b):
-            tt(V("wn", W * b, W * b + K), bank(4 + b, 0, K), V("gl", K * b, K * b + K), A.add)
+            tt(V("wn", W * b, W * b + K), bank(4 + b, 0, K), pack("gl", b), A.add)
 
-        scan(V("wsc"), V("c16"), V("ww", 0, C), 0.0, A.add, A.min)
+        firsts(1, 3)
+        places(1)
+        for b in range(3):
+            act(V("ht", b, 4 * K, 4), bank(b, 0, K), scale=0.03125)
+        if t == R - 1:
+            act(V("olr", 0, K), by(V("jj"), left))
+            act(V("olr", K, 2 * K), by(V("jj"), right))
+            dma("y", T.ol[:], lane("olr", 0))
+        put(2, 1)
+        firsts(0, 1)
+        ts(V("ht", 3, 4 * K, 4), bank(3, 0, K), 0.03125, A.mult)
+        put(1, 1)
+        places(0)
+        quant("qh", "sh", 0, K, V("ht"))
+        for b in (2, 0, 3, 1):
+            mm(4 + b, QE, 128 * b, QH, 0, K)
+        put(0, 0)
+        for b in (2, 3):
+            act(V("wn", W * b, W * b + K), bank(4 + b, 0, K), scale=-2.0)
+        scan(V("wsc"), V("ww", 0, C), V("c16"), float(LIFT), A.min, A.add)
         new(0)
         ts(V("who"), V("wsc", 15, C, 16), WF, A.add)
         new(1)
@@ -483,16 +510,15 @@ def rank_program(g, core, T, topo):
         for b in (2, 3):
             tt(V("xt", b, 4 * C, 4), by(V("wn", W * b, W * b + W), V("who")), V("tf", C * (b - 2), C * (b - 1)), A.add)
 
-    quant_state()
-    act(V("rowl", K, 2 * K), by(V("jj"), right))
+    quant_half(0)
+    quant_half(1)
     mm(0, QV, 0, QX, 0, H)
     mm(1, QV, 0, QX, H, H)
     dma("y", T.oc[:], as_(V("qx"), dt.uint8))
-    act(V("ysb", 0, H), bank(0, 0, H))
-    cp(V("ysb", H, C), bank(1, 0, H))
-    dma("s", T.y[:], V("ysb"))
-    dma("y", T.ol[:], V("rowl", parts=slice(0, 128, 16)))
     for k in range(4):
         dma("y", T.osc[4 * k:4 * k + 4, :], V("sx", parts=slice(32 * k, 32 * k + 4)))
+    cp(V("ysb", 0, H), bank(0, 0, H))
+    act(V("ysb", H, C), bank(1, 0, H))
+    dma("s", T.y[:], V("ysb"))
     plan(g, T, ops)
     g.wait_ge(T.sem.sent, sent[0])

@@ -14,11 +14,14 @@ TILE_0 = [0, 320, 576, 768, 896, 960]
 PARTS = 3
 HB = KB // PARTS
 SEG_W = [16 * (c % HB + 1) for c in range(KB)]
-SEG_0 = [sum(SEG_W[:c]) + c for c in range(KB + 1)]
-SEG_ALL = SEG_0[HB] * 16 // HB
-ON_SCALAR = (19, 18, 17, 16, 15)
-SUM_V = 9
+SEG = 16 * HB + 1
+ON_SCALAR = (19, 18, 17, 16)
+SUM_V = 11
 STEP, LIFT = 512, 16384
+FAR = 2 * C
+UNIT = 1024
+OLD = FAR + 16
+WN = K + OLD
 W = K + C
 
 BF, F32, I32, U16, U8, X4 = "bfloat16", "float32", "int32", "uint16", "uint8", "float8_e4m3fn_x4"
@@ -31,22 +34,23 @@ for _n, _w, _d in [
         ("wq", 512, X4), ("wp", 512, U8), ("lq0", 512, X4), ("lp0", 512, U8), ("lq1", 512, X4), ("lp1", 512, U8),
         ("lq2", 512, X4), ("lp2", 512, U8),
         ("ra", 32, F32), ("rat", 32, F32), ("cf", 8, F32), ("tm", 176, BF), ("jj", 320, F32), ("boi", 128, BF), ("e16", 16, BF),
-        ("k1", 176, BF), ("d0", 160, BF), ("m0", 320, BF), ("c16", 320, BF), ("pr", 320, F32),
+        ("k1", 176, BF), ("d0", 160, BF), ("m0", 320, BF), ("c16", 320, BF), ("rb", 32, F32), ("rbt", 32, F32),
         ("zz", 520, BF), ("et", 520, BF), ("qe", 512, X4), ("se", 512, U8), ("bot", 512, BF), ("qb", 128, X4), ("sb", 128, U8),
         ("g0t", 512, BF), ("qg", 128, X4), ("sg", 128, U8),
         ("u1", 320, F32), ("z", 320, F32), ("ft", 3840, BF), ("qf", 1216, X4), ("sf", 1216, U8),
         ("dsum", 320, BF), ("sgn", C * len(ON_SCALAR), BF), ("vj", 2048, BF), ("junk", 3840, BF),
-        ("rsb", 20, F32), ("rc", 20, F32), ("r1", 20, F32), ("rsc", 320, F32), ("pos", 20, U16),
+        ("rsb", 20, F32), ("rc", 20, F32), ("r1", 20, F32), ("r2", 20, F32), ("rsc", 320, F32), ("pos", 20, U16),
         ("bw", 320, BF), ("gm", 320, BF), ("pp", 320, BF), ("lr", 320, BF), ("mr", 320, BF), ("win", 336, BF), ("tr", 448, BF),
-        ("tl", 512, BF), ("ql", 128, X4), ("sl", 128, U8), ("prod", 64, BF), ("dsc", 64, BF), ("m4", 64, BF),
-        ("y0", 48, F32), ("y1", 96, F32), ("lrf", 48, F32), ("lf16", 16, U16), ("rt16", 16, U16),
-        ("wn", 4 * W, BF), ("gl", 768, BF), ("mt", 768, BF), ("qm", 192, X4), ("sm", 192, U8),
-        ("ht", 768, BF), ("qh", 192, X4), ("sh", 192, U8),
-        ("olr", 384, F32), ("ee", SEG_ALL, BF), ("md", SEG_0[KB], BF), ("kci", 8, F32), ("kp", 8, F32), ("kn", 8, F32),
-        ("es", SEG_ALL, BF), ("nl", 16, BF), ("th", 640, BF), ("tf", 640, BF), ("o16", 32, U16), ("ww", 896, F32),
+        ("tl", 512, BF), ("ql", 128, X4), ("sl", 128, U8), ("jy", FAR + 1, F32), ("fold", 16, F32),
+        ("y0", 192, F32), ("y1", 256, F32), ("ys", 192, F32), ("lrf", 16, F32), ("low", 16, F32), ("both", 16, F32),
+        ("lf16", 16, U16), ("rt16", 16, U16),
+        ("wn", 2 * WN, BF), ("wz", 2 * W, BF), ("th", 2 * OLD, BF), ("tf", 2 * C, BF), ("gl", 768, BF),
+        ("mt", 768, BF), ("qm", 192, X4), ("sm", 192, U8), ("ht", 768, BF), ("qh", 192, X4), ("sh", 192, U8),
+        ("olr", 384, F32), ("rowl", 192, F32), ("ee", SEG * KB, BF), ("md", SEG * KB, BF), ("es", SEG * KB, BF),
+        ("kci", 8, F32), ("kp", 8, F32), ("kn", 8, F32), ("o16", 16, U16), ("ww", 896, F32),
         ("wsc", 320, F32), ("who", 20, U16), ("rci", 20, F32),
-        ("g1l", 4, U16), ("g2l", 2, U16), ("endl", 2, U16), ("repi", 8, I32), ("repl", 8, U16), ("cpat", 4, F32),
-        ("rt", 160, F32), ("rtt", 160, F32), ("ysb", 320, F32)]:
+        ("g1l", 6, U16), ("g2l", 4, U16), ("repi", 8, I32), ("repl", 8, U16), ("cpat", 6, F32), ("cp2", 4, F32),
+        ("rt", 96, F32), ("rtt", 96, F32), ("ysb", 320, F32)]:
     SCRATCH[_n] = ("sbuf", [128, _w], _d)
 
 NDMA = 48
@@ -202,6 +206,9 @@ def rank_program(g, core, T, topo):
             return op("g", lambda e: e.iota(ap(out), pattern, base, cm), (), [out])
         return op("g", lambda e: e.iota(ap(out), pattern, base, cm, allow_small_or_imprecise_dtypes=True), (), [out])
 
+    def select(out, pattern, val):
+        op("g", lambda e: e.affine_select(ap(out), T.zz[:, 0:128], pattern, A.not_equal, val, 0, -1), [V("zz", 0, 128)], [out])
+
     QX, QU, QR, QV, QE, QB, QG, QF, QL, QM, QH = [("q" + x, "s" + x) for x in "xurvebgflmh"]
     sent, lands = [0], []
     for t in range(R):
@@ -218,14 +225,14 @@ def rank_program(g, core, T, topo):
            [V("wq")], (), "remote", after)
         op("g", lambda e: e.remote_dma(T["lp%d" % t][:], T.wp[:], arr, T.sem.sent, pid, rid, mask), [V("wp")], (), "remote")
 
-    Q, FIX, WF = col("rat", 0), col("rtt", 96), col("rtt", 128)
-    PF, Q256, KEEP, NT = [col("cf", i) for i in range(4)]
+    Q, WF = col("rat", 0), col("rtt", 64)
+    Q256, KEEP, NT = [col("cf", i) for i in range(3)]
 
     def tail(h):
         return V("ft", 4 * (TILE_0[h + 1] - 48), 4 * TILE_0[h + 1])
 
     def zero(q, v):
-        n = v[2].stop - v[2].start
+        n = len(range(v[2].start, v[2].stop, v[2].step))
         if q == "g":
             return iota(v, [[0, n]], 0)
         return act(v, V("zz", 0, n)) if q == "s" else dma(q, v, V("zz", 0, n))
@@ -238,17 +245,14 @@ def rank_program(g, core, T, topo):
     dma("s", V("li"), T.l[:])
     dma("s", V("mi"), T.m[:])
 
-    def pattern(name):
-        for h in range(2):
-            act(V(name, H * h, H * h + H), V("k1", 1, H + 1), F.Identity, scale=-(STEP + LIFT) / BIG, bias=float(LIFT))
-
     iota(V("ra"), [[0, 2], [1, 16]], 0)
     iota(V("repi"), [[16, 8]], 0)
     iota(V("tm"), [[0, 11], [1, 16]], 0)
     fill(V("zz"), 0.0)
-    iota(PF, [[0, 1]], 0, 1)
     iota(V("jj"), [[1, C]], 0)
+    iota(V("rb"), [[16, 2], [-STEP - 1, 16]], 16 * STEP)
     iota(V("boi"), [[16, 8], [0, 16]], 0, -1)
+    iota(V("rb", 0, 32, 16), [[16, 2]], 15 * STEP - LIFT)
     iota(V("rci"), [[16, NB]], 15)
     iota(V("rsb"), [[0, NB]], 0)
     for h in (4, 3):
@@ -257,51 +261,50 @@ def rank_program(g, core, T, topo):
         zero("y", v)
     dma("y", as_(V("wq"), dt.uint8), T.wc[:])
     dma("y", V("wp"), T.ws[:])
-    zero("y", V("g0t"))
+    for v in (V("g0t"), V("tl")):
+        zero("y", v)
     dma("y", V("vt"), T.v[:])
     turn(V("rat"), V("ra"))
     for a in (960, 1088):
         quant("qf", "sf", a, a + 128, V("zz", 0, 512))
     cp(V("repl"), V("repi"))
-    ts(KEEP, Q, 14.0, A.is_lt)
-    ts(NT, Q, 14.0, A.is_lt, -TINY, A.mult)
+    ts(KEEP, Q, 5.0, A.is_lt)
+    ts(NT, Q, 5.0, A.is_lt, -TINY, A.mult)
     for h in range(2):
         act(V("m0", H * h, H * h + H), V("tm", 0, H), F.Sign)
     ts(V("k1"), V("tm"), Q, A.not_equal, BIG, A.mult)
-    pattern("pr")
+    for h in range(2):
+        act(V("c16", H * h, H * h + H), V("k1", 1, H + 1), F.Identity, scale=-(STEP + LIFT) / BIG, bias=float(LIFT))
     ts(V("d0"), V("tm", 0, H), 0.0, A.is_equal, -BIG, A.mult)
     cp(V("l16"), V("li"))
     quant("qu", "su", 0, 128, V("ut"))
     cp(V("m16"), V("mi"))
     cp(as_(V("qr"), dt.uint32), by(as_(V("qu"), dt.uint32), V("repl")))
     act(V("sr"), by(V("su"), V("repl")))
-    act(V("lr"), by(V("jj"), V("l16")), F.Identity, bias=160.0, scale=-1.0)
+    act(V("lr"), by(V("jj"), V("l16")), F.Identity, bias=-160.0)
     act(V("mr"), by(V("jj"), V("m16")), F.Identity, bias=160.0, scale=-1.0)
-    iota(V("rt", 96, 128), [[16, 2], [-STEP - 1, 16]], 16 * STEP)
-    iota(V("rt", 128, 160), [[0, 2], [-STEP, 16]], 16 * STEP)
-    iota(V("rt", 0, 16), [[32, 2], [192, 2], [1, 4]], 1)
-    iota(V("rt", 16, 32), [[32, 2], [192, 2], [1, 4]], 17)
+    iota(V("rt", 64, 96), [[0, 2], [-STEP, 16]], 16 * STEP)
+    iota(V("rt", 0, 32), [[16, 2], [192, 2], [1, 8]], 1)
     iota(V("rt", 32, 64), [[16, 2], [32, 8], [192, 2]], 14)
-    iota(V("rt", 96, 128, 16), [[16, 2]], 15 * STEP - LIFT)
-    iota(V("rt", 128, 160, 16), [[0, 2]], 15 * STEP - LIFT)
-    for c in range(HB):
-        iota(V("rt", 64 + c, 96, HB), [[0, 2], [SEG_0[HB], 16 // HB]], SEG_0[c + 1] - 1)
-    iota(V("cpat"), [[64, 4]], 0)
+    iota(V("rt", 64, 96, 16), [[0, 2]], 15 * STEP - LIFT)
+    iota(V("cpat"), [[32, 6]], 0)
+    iota(V("cp2"), [[1, 2], [0, 2]], 0)
+    select(V("et", 3, 515, 4), [[1, 128]], -0.5)
     iota(V("kci"), [[16, 8]], 128)
-    iota(V("m4"), [[0, 64]], 1)
-    iota(V("y0", 0, 48, 3), [[0, 16]], 0)
-    iota(V("m4", 0, 64, 4), [[0, 16]], 0)
-    iota(V("y0", 2, 48, 3), [[0, 16]], -1)
-    for v in (V("win"), V("md", 0, SEG_0[HB]), V("tr", 384, 448)):
+    iota(V("y0", 0, 192, 2), [[0, 96]], 0)
+    iota(V("y1", 0, 192), [[0, 192]], 64 * UNIT)
+    iota(V("y0", 0, 192, 16), [[0, KB]], 64 * UNIT)
+    iota(V("y1", 0, 192, 16), [[0, KB]], 2 * UNIT)
+    for v in (V("win"), V("md", 0, SEG * HB), V("tr", 384, 448), V("wn", K + C, 2 * WN, WN), V("th", C, 2 * OLD, OLD)):
         zero("g", v)
 
     def late(part):
         if part == "block ones":
             for s in range(4):
                 ts(V("bot", s, 512, 4), V("boi"), Q, A.add, 0.0, A.is_equal)
-            ts(V("rc"), V("rci"), col("pr", 15), A.add)
-        if part == "identity":
-            ts(V("et", 3, 515, 4), V("jj", 0, 128), PF, A.is_equal, -0.5, A.mult)
+            turn(V("rbt"), V("rb"))
+        if part == "places":
+            ts(V("rc"), V("rci"), col("rbt", 0), A.add)
         if part == "ones":
             quant("qb", "sb", 0, 128, V("bot"))
         if part == "lists":
@@ -310,26 +313,21 @@ def rank_program(g, core, T, topo):
             quant("qe", "se", 128 * part, 128 * part + 128, V("et", 3 - part, 515 - part))
             unpack(part)
         if part == "signs":
-            ts(V("g0t", 0, 512, 4), V("tm", 0, 128), PF, A.is_equal)
             ts(V("g1l"), V("cpat"), col("rtt", 0), A.add)
         if part == "group 0":
             quant("qg", "sg", 0, 128, V("g0t"))
-            ts(V("g2l"), V("jj", 0, 2), col("rtt", 32), A.add)
-        if part == "ends":
-            cp(col("endl", 0), col("rtt", 64))
+            ts(V("g2l"), V("cp2"), col("rtt", 32), A.add)
         if part == "firsts":
-            pattern("c16")
             act(V("e16"), V("k1", 0, 16), F.Sign)
             act(Q256, Q, scale=1.0 / 256)
             act(V("kp"), V("kci"), F.Identity, scale=1.0 / 256, bias=Q256)
             act(V("kn"), V("kp"), scale=-1.0)
             for c in range(HB):
-                act(V("md", SEG_0[c + 1] - 17, SEG_0[c + 1] - 1), V("e16"), F.Identity, bias=col("kn", c), scale=col("kp", c))
-            for c in range(HB):
-                act(col("md", SEG_0[c + 1] - 1), col("zz", 0), F.Identity, bias=0.25)
-                act(col("md", SEG_0[c]), col("zz", 0), F.Identity, bias=4.0)
+                act(V("md", SEG * (c + 1) - 17, SEG * (c + 1) - 1), V("e16"), F.Identity, bias=col("kn", c), scale=col("kp", c))
+            act(V("md", SEG - 1, SEG * HB, SEG), V("zz", 0, HB), F.Identity, bias=0.25)
+            act(V("md", 0, SEG * HB, SEG), V("zz", 0, HB), F.Identity, bias=4.0)
             for h in range(1, PARTS):
-                act(V("md", h * SEG_0[HB], (h + 1) * SEG_0[HB]), V("md", 0, SEG_0[HB]))
+                act(V("md", h * SEG * HB, (h + 1) * SEG * HB), V("md", 0, SEG * HB))
 
     def slot(c, n, name="ft"):
         h, s = divmod(NB - c, 4)
@@ -352,8 +350,9 @@ def rank_program(g, core, T, topo):
     def unpack(b):
         mm(4 + b, QE, 128 * b, QX, 0, C)
 
-    def old(b):
-        return V("wn", W * b + K, W * b + W) if b < 2 else V("th", C * (b - 2), C * (b - 1))
+    def old(b, a=0, z=FAR + 1, step=1):
+        name, at = ("wn", WN * b + K) if b < 2 else ("th", OLD * (b - 2))
+        return V(name, at + a, at + z, step)
 
     def pack(name, b):
         return V(name, K * b, K * b + K)
@@ -379,10 +378,14 @@ def rank_program(g, core, T, topo):
         rows = [dma("y", lane("gm", 14), lane("lr", 14)), dma("y", lane("gm", 15), lane("mr", 15))]
         if t == 0:
             send(0, rows)
-            for v in (V("tl"), V("es"), V("wn", 2 * W + K, 3 * W), V("wn", 3 * W + K, 4 * W)):
-                zero("g", v)
+            select(V("g0t", 0, 512, 4), [[0, 8], [1, 16]], float(UNIT))
+            iota(V("jy", 0, C), [[-1, C]], C)
+            iota(V("jy", C, FAR + 1), [[1, C + 1]], 0)
+            iota(V("ee"), [[0, SEG * KB]], 2)
         iota(V("ww", 0, C), [[1, C]], K)
         if t == 0:
+            for b in range(2):
+                zero("g", V("wz", W * b + K, W * b + W))
             send(1)
             send(2)
         for x in range(len(ON_SCALAR) + 1):
@@ -394,14 +397,14 @@ def rank_program(g, core, T, topo):
                 act(slot(c, 16 * c), V("sgn", C * (x - 1), C * (x - 1) + 16 * c), F.Relu, accum_out=col("rsb", c))
         for c in range(1, ON_SCALAR[-1]):
             ts(slot(c, 16 * c), bank(0, 0, 16 * c), col("z", 16 * c + 15), A.is_lt)
-            if c == 2:
+            if c == 3:
                 tt(slot(NB, C), V("z"), bank(0, 0, C), A.is_ge)
-            if c == 4:
+            if c == 6:
                 scan(V("dsum"), V("m0"), slot(NB, C), 0.0, A.mult, A.add)
-                first("identity")
-            if c == 5:
-                tt(V("r1"), V("rc"), V("dsum", 15, C, 16), A.subtract)
+                first("places")
             if c == 9:
+                tt(V("r1"), V("rc"), V("dsum", 15, C, 16), A.subtract)
+            if c == 10:
                 first("ones")
                 qtile(3, 5)
                 sum_tile(4, first=True)
@@ -409,23 +412,20 @@ def rank_program(g, core, T, topo):
         for c in range(1, SUM_V):
             act(slot(c, 16 * c, "junk"), slot(c, 16 * c), F.Identity, accum_out=col("rsb", c))
         row_sum(SUM_V)
-        qtile(2, 3)
-        sum_tile(2)
-        row_sum(SUM_V + 1)
-        qtile(0, 1)
-        sum_tile(0)
-        for c in range(SUM_V + 2, ON_SCALAR[-1]):
+        for h in (2, 0, 1):
+            qtile(h, h + 1)
+            sum_tile(h, last=h == 1)
+        for c in range(SUM_V + 1, ON_SCALAR[-1]):
             row_sum(c)
-        qtile(1, 2)
-        sum_tile(1, last=True)
+        tt(V("pp", 0, K), by(V("bw"), V("l16", 0, KB)), V("gm", 0, K), A.subtract)
         mine = V("r1", SUM_V, ON_SCALAR[-1])
         tt(mine, mine, V("vj", 2032 + SUM_V, 2032 + ON_SCALAR[-1]), A.subtract)
-        tt(V("pp"), by(V("bw"), V("l16")), V("gm"), A.subtract)
-        tt(V("pr", 15, C, 16), V("r1"), V("rsb"), A.subtract)
         first("lists")
-        scan(V("rsc"), bank(3, 0, C), V("pr"), float(LIFT), A.min, A.add)
+        scan(V("rsc"), bank(3, 0, C), V("c16"), float(LIFT), A.min, A.add)
+        tt(V("r2"), V("r1"), V("rsb"), A.subtract)
+        tt(V("pp", K, C), by(V("bw"), V("l16", KB, NB)), V("gm", K, C), A.subtract)
         first(2)
-        ts(V("pos"), V("rsc", 15, C, 16), FIX, A.add)
+        tt(V("pos"), V("rsc", 15, C, 16), V("r2"), A.add)
         first(3)
         cp(by(V("win"), V("pos")), V("pp"))
         first(0)
@@ -435,90 +435,94 @@ def rank_program(g, core, T, topo):
         first(1)
         first("firsts")
         for b in (2, 3, 0, 1):
-            act(old(b), bank(4 + b, 0, C))
-        for b in (2, 3):
-            act(V("tf", C * (b - 2), C * (b - 1)), bank(4 + b, 0, C), scale=-2.0)
-        cp(V("tl", 0, 256, 4), by(V("tr"), V("g1l")))
+            act(old(b, 0, C), bank(4 + b, 0, C))
+            act(old(b, FAR, C, -1), bank(4 + b, 0, C))
+        cp(V("tl", 0, 384, 4), by(V("tr"), V("g1l")))
         first("group 0")
         quant("ql", "sl", 0, 128, V("tl"))
-        ts(V("y1", 1, 96, 3), by(V("tr"), V("g2l")), 160.0, A.add)
+        ts(V("y1", 8, 256, 16), by(V("tr"), V("g2l", 0, 1)), FAR - 160.0, A.add)
+        ts(V("low"), by(V("tr"), V("g2l", 2, 3)), 160.0, A.add)
         mm(0, QG, 0, QL, 0, 128)
-        first("ends")
-        tt(V("y0", 1, 48, 3), V("y1", 49, 96, 3), V("y1", 1, 48, 3), A.subtract)
-        tt(V("y1", 2, 48, 3), V("y1", 49, 96, 3), V("y1", 1, 48, 3), A.add)
+        tt(V("both"), V("y1", 8, 256, 16), V("low"), A.add)
         if t == 1:
             quant("qv", "sv", 0, 128, V("vt"))
-        tt(V("prod"), bank(0, 0, 64), V("tl", 0, 256, 4), A.mult)
-        scan(V("dsc"), V("m4"), V("prod"), 0.0, A.mult, A.add)
-        ts(V("y1", 0, 48, 3), V("dsc", 3, 64, 4), 0.0, A.is_lt)
-        scan(V("lrf"), V("y0"), V("y1", 0, 48), 0.0, A.mult, A.add)
-        cp(V("lf16"), V("lrf", 1, 48, 3))
-        cp(V("rt16"), V("lrf", 2, 48, 3))
+        tt(V("y0", 1, 192, 2), bank(0, 0, 96), V("tl", 0, 384, 4), A.mult)
+        scan(V("ys"), V("y0"), V("y1", 0, 192), 0.0, A.add, A.min)
         left, right = V("lf16", 0, KB), V("rt16", 0, KB)
-        for b in range(3):
-            act(pack("gl", b), by(old(b), left))
-        ts(V("nl"), V("lrf", 1, 48, 3), 160.0, A.subtract, -1.0 / 1024, A.mult)
+        tt(left, V("ys", 8, 192, 16), V("low", 0, KB), A.max)
+        tt(V("lrf", 0, KB), V("ys", 8, 192, 16), V("low", 0, KB), A.max)
+        act(pack("gl", 0), by(old(0), left))
+        act(V("fold", 0, KB), V("lrf", 0, KB), F.Abs, bias=-float(C))
+        act(pack("gl", 1), by(old(1), left))
+        act(V("ee", SEG - 1, SEG * KB, SEG), V("fold", 0, KB), F.Identity, scale=1.0 / 1024, bias=(160.0 - C) / 1024)
+        act(pack("gl", 2), by(old(2), left))
         cp(pack("gl", 3), by(old(3), left))
-        cp(by(V("ee"), col("endl", 0)), V("nl"))
+        tt(right, V("both", 0, KB), V("lrf", 0, KB), A.subtract)
+        cp(V("rowl"), by(V("jy"), left))
         for h in range(PARTS - 1, -1, -1):
             for c in range(HB * h, HB * h + HB):
-                act(V("ee", SEG_0[c], SEG_0[c + 1] - 1), by(V("jj"), V("lf16", HB * h, c + 1)), F.Abs, bias=col("lrf", 3 * c + 1), scale=-1.0)
+                act(V("ee", SEG * (c + 1) - 1 - SEG_W[c], SEG * (c + 1) - 1), V("rowl", 16 * HB * h, 16 * (c + 1)), F.Abs,
+                    bias=col("fold", c), scale=-1.0)
         for b in (3, 0, 1, 2):
             tt(V("mt", b, 4 * K, 4), by(old(b), right), pack("gl", b), A.subtract)
+
+        def firsts(h0, h1):
+            a, b = SEG * HB * h0, SEG * HB * h1
+            scan(V("es", a, b), V("md", a, b), V("ee", a, b), 2.0, A.add, A.min)
+
+        def places(h0, h1):
+            ts(V("o16", HB * h0, HB * h1), V("es", SEG * (HB * h0 + 1) - 1, SEG * HB * h1, SEG), -1024.0, A.mult, 160.0, A.add)
+
+        def put(h):
+            cp(by(V("ww"), V("o16", HB * h, HB * h + HB)), V("jj", 16 * HB * h, 16 * HB * (h + 1)))
+
+        def new(b):
+            tt(V("wn", WN * b, WN * b + K), bank(4 + b, 0, K), pack("gl", b), A.add)
+
+        firsts(1, 3)
         quant("qm", "sm", 0, K, V("mt"))
         for b in range(4):
             mm(b, ("lq%d" % t, "lp%d" % t), 128 * b, QM, 0, K, ext=[("arr%d" % t, lands[t])] if b == 0 else ())
-
-        def firsts(h0, h1):
-            a, b = SEG_0[HB * h0], SEG_0[HB * h1]
-            scan(V("es", a, b), V("md", a, b), V("ee", a, b), 2.0, A.add, A.min)
-
-        def places(x):
-            ts(V("o16", 16 * x, 16 * x + 16), by(V("es"), col("endl", 0)), -1024.0, A.mult, 160.0, A.add)
-
-        def put(h, x):
-            cp(by(V("ww"), V("o16", 16 * x + HB * h, 16 * x + HB * h + HB)), V("jj", 16 * HB * h, 16 * HB * (h + 1)))
-
-        def new(b):
-            tt(V("wn", W * b, W * b + K), bank(4 + b, 0, K), pack("gl", b), A.add)
-
-        firsts(1, 3)
-        places(1)
+        places(1, 3)
+        firsts(0, 1)
+        put(2)
+        places(0, 1)
         for b in range(3):
             act(V("ht", b, 4 * K, 4), bank(b, 0, K), scale=0.03125)
+        for b in (2, 3):
+            act(V("tf", C * (b - 2), C * (b - 1)), old(b, 0, C), scale=-2.0)
         if t == R - 1:
-            act(V("olr", 0, K), by(V("jj"), left))
-            act(V("olr", K, 2 * K), by(V("jj"), right))
+            act(V("olr", 0, K), V("rowl"), F.Identity, scale=-1.0, bias=float(C))
+            act(V("olr", K, 2 * K), by(V("jy"), right), F.Identity, scale=-1.0, bias=float(C))
             dma("y", T.ol[:], lane("olr", 0))
-        put(2, 1)
-        firsts(0, 1)
+        put(1)
         ts(V("ht", 3, 4 * K, 4), bank(3, 0, K), 0.03125, A.mult)
-        put(1, 1)
-        places(0)
+        put(0)
         quant("qh", "sh", 0, K, V("ht"))
         for b in (2, 0, 3, 1):
             mm(4 + b, QE, 128 * b, QH, 0, K)
-        put(0, 0)
-        for b in (2, 3):
-            act(V("wn", W * b, W * b + K), bank(4 + b, 0, K), scale=-2.0)
         scan(V("wsc"), V("ww", 0, C), V("c16"), float(LIFT), A.min, A.add)
-        new(0)
+        for b in (2, 3):
+            act(V("wz", W * (b - 2), W * (b - 2) + K), bank(4 + b, 0, K), scale=-2.0)
         ts(V("who"), V("wsc", 15, C, 16), WF, A.add)
+        new(0)
         new(1)
         for b in (0, 1):
-            act(V("xt", b, 4 * C, 4), by(V("wn", W * b, W * b + W), V("who")), scale=-2.0)
+            act(V("xt", b, 4 * C, 4), by(V("wn", WN * b, WN * b + W), V("who")), scale=-2.0)
         for b in (2, 3):
-            tt(V("xt", b, 4 * C, 4), by(V("wn", W * b, W * b + W), V("who")), V("tf", C * (b - 2), C * (b - 1)), A.add)
+            tt(V("xt", b, 4 * C, 4), by(V("wz", W * (b - 2), W * (b - 1)), V("who")), V("tf", C * (b - 2), C * (b - 1)), A.add)
 
     quant_half(0)
     quant_half(1)
     mm(0, QV, 0, QX, 0, H)
     mm(1, QV, 0, QX, H, H)
-    dma("y", T.oc[:], as_(V("qx"), dt.uint8))
+    dma("s", T.oc[:, 0:4 * H], as_(V("qx", 0, H), dt.uint8))
+    dma("y", T.oc[:, 4 * H:4 * C], as_(V("qx", H, C), dt.uint8))
     for k in range(4):
         dma("y", T.osc[4 * k:4 * k + 4, :], V("sx", parts=slice(32 * k, 32 * k + 4)))
     cp(V("ysb", 0, H), bank(0, 0, H))
     act(V("ysb", H, C), bank(1, 0, H))
-    dma("s", T.y[:], V("ysb"))
+    dma("y", T.y[:, 0:H], V("ysb", 0, H))
+    dma("s", T.y[:, H:C], V("ysb", H, C))
     plan(g, T, ops)
     g.wait_ge(T.sem.sent, sent[0])

import numpy as np
from concourse.mybir import dt, AluOpType, ActivationFunctionType

A = AluOpType
F = ActivationFunctionType
C, K, R, N = 320, 192, 3, 4
H = C // 2
BIG = 2.0 ** 90
TINY = 2.0 ** -110
NB = C // 16
KB = K // 16
TILE_W = [320, 256, 192, 128, 64]
TILE_0 = [0, 320, 576, 768, 896, 960]
PARTS = 3
HB = KB // PARTS
SEG_W = [16 * (c % HB + 1) for c in range(KB)]
SEG = 16 * HB + 1
ON_SCALAR = (19, 18, 17, 16)
SUM_V = 11
STEP, LIFT = 512, 16384
FAR = 2 * C
UNIT = 1024
OLD = FAR + 16
WN = K + OLD
W = K + C

BF, F32, I32, U16, U8, X4 = "bfloat16", "float32", "int32", "uint16", "uint8", "float8_e4m3fn_x4"
SCRATCH = {"ps": ("psum", [128, 4096], F32)}
for _n, _w, _d in [
        ("xt", 1280, BF), ("qx", 320, X4), ("sx", 320, U8),
        ("ut", 512, BF), ("qu", 128, X4), ("su", 128, U8), ("qr", 128, X4), ("sr", 128, U8),
        ("vt", 512, BF), ("qv", 128, X4), ("sv", 128, U8),
        ("li", 20, I32), ("mi", 20, I32), ("l16", 20, U16), ("m16", 20, U16),
        ("wq", 512, X4), ("wp", 512, U8), ("lq0", 512, X4), ("lp0", 512, U8), ("lq1", 512, X4), ("lp1", 512, U8),
        ("lq2", 512, X4), ("lp2", 512, U8),
        ("ra", 32, F32), ("rat", 32, F32), ("cf", 8, F32), ("tm", 176, BF), ("jj", 320, F32), ("boi", 128, BF), ("e16", 16, BF),
        ("k1", 176, BF), ("d0", 160, BF), ("m0", 320, BF), ("c16", 320, BF), ("rb", 32, F32), ("rbt", 32, F32),
        ("zz", 520, BF), ("et", 520, BF), ("qe", 512, X4), ("se", 512, U8), ("bot", 512, BF), ("qb", 128, X4), ("sb", 128, U8),
        ("g0t", 512, BF), ("qg", 128, X4), ("sg", 128, U8),
        ("u1", 320, F32), ("z", 320, F32), ("ft", 3840, BF), ("qf", 1216, X4), ("sf", 1216, U8),
        ("dsum", 320, BF), ("sgn", C * len(ON_SCALAR), BF), ("vj", 2048, BF), ("junk", 3840, BF),
        ("rsb", 20, F32), ("rc", 20, F32), ("r1", 20, F32), ("r2", 20, F32), ("rsc", 320, F32), ("pos", 20, U16),
        ("bw", 320, BF), ("gm", 320, BF), ("pp", 320, BF), ("lr", 320, BF), ("mr", 320, BF), ("win", 336, BF), ("tr", 448, BF),
        ("tl", 512, BF), ("ql", 128, X4), ("sl", 128, U8), ("jy", FAR + 1, F32), ("fold", 16, F32),
        ("y0", 192, F32), ("y1", 256, F32), ("ys", 192, F32), ("lrf", 16, F32), ("low", 16, F32), ("both", 16, F32),
        ("lf16", 16, U16), ("rt16", 16, U16),
        ("wn", 2 * WN, BF), ("wz", 2 * W, BF), ("th", 2 * OLD, BF), ("tf", 2 * C, BF), ("gl", 768, BF),
        ("mt", 768, BF), ("qm", 192, X4), ("sm", 192, U8), ("ht", 768, BF), ("qh", 192, X4), ("sh", 192, U8),
        ("olr", 384, F32), ("rowl", 192, F32), ("ee", SEG * KB, BF), ("md", SEG * KB, BF), ("es", SEG * KB, BF),
        ("kci", 8, F32), ("kp", 8, F32), ("kn", 8, F32), ("o16", 16, U16), ("ww", 896, F32),
        ("wsc", 320, F32), ("who", 20, U16), ("rci", 20, F32),
        ("g1l", 6, U16), ("g2l", 4, U16), ("repi", 8, I32), ("repl", 8, U16), ("cpat", 6, F32), ("cp2", 4, F32),
        ("rt", 96, F32), ("rtt", 96, F32), ("ysb", 320, F32)]:
    SCRATCH[_n] = ("sbuf", [128, _w], _d)

NDMA = 48
SEMAPHORES = ["cv", "cs", "ct", "cg", "arr0", "arr1", "arr2", "sent"] + ["d%d" % i for i in range(NDMA)]
ENGINE_SEM = {"v": "cv", "s": "cs", "t": "ct", "g": "cg"}
ALL = slice(0, 128)


def V(name, a=0, b=None, step=1, parts=ALL):
    return (name, parts, slice(a, SCRATCH[name][1][1] if b is None else b, step), None, None)


def col(name, a):
    return V(name, a, a + 1)


def by(win, off):
    return win[:4] + (off,)


def as_(v, d):
    return v[:3] + (d, v[4])


def bank(b, a, n):
    return V("ps", 512 * b + a, 512 * b + n)


def is_view(v):
    return isinstance(v, tuple)


def plan(g, T, ops):
    queue = {"v": g.vector, "s": g.scalar, "t": g.tensor, "g": g, "y": g.sync}
    wrote = {n: np.full((1, 8) if n == "ps" else s[1], -1) for n, s in SCRATCH.items()}
    read = {n: {} for n in SCRATCH}
    known, ndma = {q: {} for q in queue}, 0

    def at(v):
        return (slice(0, 1), slice(v[2].start // 512, v[2].start // 512 + 1)) if v[0] == "ps" else (v[1], v[2])

    for i, o in enumerate(ops):
        q = o["q"]
        if o["kind"] == "dma":
            o["key"] = "d%d" % ndma
            ndma += 1
        else:
            o["key"] = q
        reads = [v for v in o["r"] if is_view(v)]
        reads += [v[4] for v in reads + o["w"] if v[4] is not None]
        deps = set(o["after"])
        for v in reads:
            deps.update(np.unique(wrote[v[0]][at(v)]).tolist())
            if v[0] == "ps":
                deps.update(int(m[at(v)].max()) for k, m in read["ps"].items() if k != q)
        for v in o["w"]:
            if v[0] != "ps":
                deps.update(np.unique(wrote[v[0]][at(v)]).tolist())
            deps.update(int(m[at(v)].max()) for m in read[v[0]].values())
        for v in reads:
            read[v[0]].setdefault(o["key"], np.full(wrote[v[0]].shape, -1))[at(v)] = i
        for v in o["w"]:
            wrote[v[0]][at(v)] = i
        deps.discard(-1)
        deps.discard(i)
        o["waits"] = []
        for j in sorted(deps, reverse=True):
            d = ops[j]
            if known[q].get(d["key"], -1) >= j:
                continue
            o["waits"].append(j)
            d["inc"] = True
            for k, val in d["clock"].items():
                known[q][k] = max(known[q].get(k, -1), val)
        o["clock"] = dict(known[q])
        o["clock"][o["key"]] = i
    count = {q: 0 for q in ENGINE_SEM}
    for o in ops:
        e = queue[o["q"]]
        for j in o["waits"]:
            e.wait_ge(T.sem[ops[j]["sem"]], ops[j]["val"])
        for name, val in o["ext"]:
            e.wait_ge(T.sem[name], val)
        ins = o["fn"](e)
        if o["kind"] == "dma":
            o["sem"], o["val"] = o["key"], 16
            ins.then_inc(T.sem[o["sem"]], 16)
        elif o["kind"] == "op" and o.get("inc"):
            count[o["q"]] += 1
            o["sem"], o["val"] = ENGINE_SEM[o["q"]], count[o["q"]]
            ins.then_inc(T.sem[o["sem"]], 1)
    for o in ops:
        if o["kind"] == "dma" and not o.get("inc"):
            queue[o["q"]].wait_ge(T.sem[o["sem"]], 16)


def rank_program(g, core, T, topo):
    rank = T.rank_of(core)
    if rank is None:
        return
    ops = []

    def ap(v):
        if not is_view(v):
            return v
        x = T[v[0]][v[1], v[2]]
        if v[3] is not None:
            x = x.bitcast(v[3])
        return x if v[4] is None else x.indirect(ap(v[4]))

    def op(q, fn, r=(), w=(), kind="op", after=(), ext=()):
        ops.append({"q": q, "fn": fn, "r": list(r), "w": [v for v in w if is_view(v)], "kind": kind, "after": list(after), "ext": list(ext)})
        return len(ops) - 1

    def dma(q, out, in_):
        return op(q, lambda e: e.dma_start(ap(out), ap(in_)), [in_], [out], "dma")

    def ts(out, in0, s1, o0, s2=None, o1=None):
        if o1 is None:
            return op("v", lambda e: e.tensor_scalar(ap(out), ap(in0), ap(s1), None, o0), [in0, s1], [out])
        return op("v", lambda e: e.tensor_scalar(ap(out), ap(in0), ap(s1), ap(s2), o0, o1), [in0, s1, s2], [out])

    def tt(out, a, b, o):
        return op("v", lambda e: e.tensor_tensor(ap(out), ap(a), ap(b), o), [a, b], [out])

    def cp(out, a):
        return op("v", lambda e: e.tensor_copy(ap(out), ap(a)), [a], [out])

    def scan(out, a, b, init, o0, o1):
        return op("v", lambda e: e.tensor_tensor_scan(ap(out), ap(a), ap(b), init, o0, o1), [a, b], [out])

    def turn(out, a):
        return op("v", lambda e: e.transpose(ap(out), ap(a)), [a], [out])

    def fill(out, val):
        return op("v", lambda e: e.memset(ap(out), val), (), [out])

    def quant(q, s, a, b, src):
        return op("v", lambda e: e.quantize_mx(ap(V(q, a, b)), ap(V(s, a, b)), ap(src)), [src], [V(q, a, b), V(s, a, b)])

    def act(out, a, func=F.Copy, **kw):
        acc = kw.get("accum_out")
        return op("s", lambda e: e.activation(ap(out), ap(a), func, **{k: ap(x) for k, x in kw.items()}),
                  [a, kw.get("bias"), kw.get("scale")], [out, acc])

    def mm(b, left, a, right, c, n, start=True, stop=True, ext=()):
        v = [V(left[0], a, a + 128), V(left[1], a, a + 128), V(right[0], c, c + n), V(right[1], c, c + n)]
        return op("t", lambda e: e.matmul_mx(ap(bank(b, 0, n)), ap(v[0]), ap(v[1]), ap(v[2]), ap(v[3]), start, stop), v,
                  [bank(b, 0, n)], ext=ext)

    def iota(out, pattern, base, cm=0):
        if SCRATCH[out[0]][2] == I32:
            return op("g", lambda e: e.iota(ap(out), pattern, base, cm), (), [out])
        return op("g", lambda e: e.iota(ap(out), pattern, base, cm, allow_small_or_imprecise_dtypes=True), (), [out])

    def select(out, pattern, val):
        op("g", lambda e: e.affine_select(ap(out), T.zz[:, 0:128], pattern, A.not_equal, val, 0, -1), [V("zz", 0, 128)], [out])

    QX, QU, QR, QV, QE, QB, QG, QF, QL, QM, QH = [("q" + x, "s" + x) for x in "xurvebgflmh"]
    sent, lands = [0], []
    for t in range(R):
        src = T.cores[(rank + 1 + t) % N]
        lands.append(2 * len(topo.engines(src, core)))

    def send(t, after=()):
        dst = T.cores[(rank - 1 - t) % N]
        rid, pid, _ = topo.addr(dst)
        mask = topo.mask(core, dst)
        sent[0] += 2 * len(topo.engines(core, dst))
        arr = T.sem["arr%d" % t]
        op("g", lambda e: e.remote_dma(T["lq%d" % t][:].bitcast(dt.uint8), T.wq[:].bitcast(dt.uint8), arr, T.sem.sent, pid, rid, mask),
           [V("wq")], (), "remote", after)
        op("g", lambda e: e.remote_dma(T["lp%d" % t][:], T.wp[:], arr, T.sem.sent, pid, rid, mask), [V("wp")], (), "remote")

    Q, WF = col("rat", 0), col("rtt", 64)
    Q256, KEEP, NT = [col("cf", i) for i in range(3)]

    def tail(h):
        return V("ft", 4 * (TILE_0[h + 1] - 48), 4 * TILE_0[h + 1])

    def zero(q, v):
        n = len(range(v[2].start, v[2].stop, v[2].step))
        if q == "g":
            return iota(v, [[0, n]], 0)
        return act(v, V("zz", 0, n)) if q == "s" else dma(q, v, V("zz", 0, n))

    def lane(name, q):
        return V(name, parts=slice(q, 128, 16))

    dma("y", V("ut"), T.u[:])
    dma("y", V("xt"), T.x[:])
    dma("s", V("li"), T.l[:])
    dma("s", V("mi"), T.m[:])

    iota(V("ra"), [[0, 2], [1, 16]], 0)
    iota(V("repi"), [[16, 8]], 0)
    iota(V("tm"), [[0, 11], [1, 16]], 0)
    fill(V("zz"), 0.0)
    iota(V("jj"), [[1, C]], 0)
    iota(V("rb"), [[16, 2], [-STEP - 1, 16]], 16 * STEP)
    iota(V("boi"), [[16, 8], [0, 16]], 0, -1)
    iota(V("rb", 0, 32, 16), [[16, 2]], 15 * STEP - LIFT)
    iota(V("rci"), [[16, NB]], 15)
    iota(V("rsb"), [[0, NB]], 0)
    for h in (4, 3):
        zero("s", tail(h))
    for v in (tail(0), tail(2), tail(1), V("et")):
        zero("y", v)
    dma("y", as_(V("wq"), dt.uint8), T.wc[:])
    dma("y", V("wp"), T.ws[:])
    for v in (V("g0t"), V("tl")):
        zero("y", v)
    dma("y", V("vt"), T.v[:])
    turn(V("rat"), V("ra"))
    for a in (960, 1088):
        quant("qf", "sf", a, a + 128, V("zz", 0, 512))
    cp(V("repl"), V("repi"))
    ts(KEEP, Q, 5.0, A.is_lt)
    ts(NT, Q, 5.0, A.is_lt, -TINY, A.mult)
    for h in range(2):
        act(V("m0", H * h, H * h + H), V("tm", 0, H), F.Sign)
    ts(V("k1"), V("tm"), Q, A.not_equal, BIG, A.mult)
    for h in range(2):
        act(V("c16", H * h, H * h + H), V("k1", 1, H + 1), F.Identity, scale=-(STEP + LIFT) / BIG, bias=float(LIFT))
    ts(V("d0"), V("tm", 0, H), 0.0, A.is_equal, -BIG, A.mult)
    cp(V("l16"), V("li"))
    quant("qu", "su", 0, 128, V("ut"))
    cp(V("m16"), V("mi"))
    cp(as_(V("qr"), dt.uint32), by(as_(V("qu"), dt.uint32), V("repl")))
    act(V("sr"), by(V("su"), V("repl")))
    act(V("lr"), by(V("jj"), V("l16")), F.Identity, bias=-160.0)
    act(V("mr"), by(V("jj"), V("m16")), F.Identity, bias=160.0, scale=-1.0)
    iota(V("rt", 64, 96), [[0, 2], [-STEP, 16]], 16 * STEP)
    iota(V("rt", 0, 32), [[16, 2], [192, 2], [1, 8]], 1)
    iota(V("rt", 32, 64), [[16, 2], [32, 8], [192, 2]], 14)
    iota(V("rt", 64, 96, 16), [[0, 2]], 15 * STEP - LIFT)
    iota(V("cpat"), [[32, 6]], 0)
    iota(V("cp2"), [[1, 2], [0, 2]], 0)
    select(V("et", 3, 515, 4), [[1, 128]], -0.5)
    iota(V("kci"), [[16, 8]], 128)
    iota(V("y0", 0, 192, 2), [[0, 96]], 0)
    iota(V("y1", 0, 192), [[0, 192]], 64 * UNIT)
    iota(V("y0", 0, 192, 16), [[0, KB]], 64 * UNIT)
    iota(V("y1", 0, 192, 16), [[0, KB]], 2 * UNIT)
    for v in (V("win"), V("md", 0, SEG * HB), V("tr", 384, 448), V("wn", K + C, 2 * WN, WN), V("th", C, 2 * OLD, OLD)):
        zero("g", v)

    def late(part):
        if part == "block ones":
            for s in range(4):
                ts(V("bot", s, 512, 4), V("boi"), Q, A.add, 0.0, A.is_equal)
            turn(V("rbt"), V("rb"))
        if part == "places":
            ts(V("rc"), V("rci"), col("rbt", 0), A.add)
        if part == "ones":
            quant("qb", "sb", 0, 128, V("bot"))
        if part == "lists":
            turn(V("rtt"), V("rt"))
        if part in range(4):
            quant("qe", "se", 128 * part, 128 * part + 128, V("et", 3 - part, 515 - part))
            unpack(part)
        if part == "signs":
            ts(V("g1l"), V("cpat"), col("rtt", 0), A.add)
        if part == "group 0":
            quant("qg", "sg", 0, 128, V("g0t"))
            ts(V("g2l"), V("cp2"), col("rtt", 32), A.add)
        if part == "firsts":
            act(V("e16"), V("k1", 0, 16), F.Sign)
            act(Q256, Q, scale=1.0 / 256)
            act(V("kp"), V("kci"), F.Identity, scale=1.0 / 256, bias=Q256)
            act(V("kn"), V("kp"), scale=-1.0)
            for c in range(HB):
                act(V("md", SEG * (c + 1) - 17, SEG * (c + 1) - 1), V("e16"), F.Identity, bias=col("kn", c), scale=col("kp", c))
            act(V("md", SEG - 1, SEG * HB, SEG), V("zz", 0, HB), F.Identity, bias=0.25)
            act(V("md", 0, SEG * HB, SEG), V("zz", 0, HB), F.Identity, bias=4.0)
            for h in range(1, PARTS):
                act(V("md", h * SEG * HB, (h + 1) * SEG * HB), V("md", 0, SEG * HB))

    def slot(c, n, name="ft"):
        h, s = divmod(NB - c, 4)
        a = 4 * TILE_0[h] + s
        return V(name, a, a + 4 * n - 3, 4)

    def qtile(h, k):
        quant("qf", "sf", TILE_0[h], TILE_0[k], V("ft", 4 * TILE_0[h], 4 * TILE_0[k]))

    def sum_tile(h, first=False, last=False):
        mm(3, QB, 0, QF, TILE_0[h], C if first else TILE_W[h], first, last)

    def row_sum(c):
        n, a = 8 * c, slot(c, 16 * c)[2].start
        scan(V("vj", 16 * (128 - n) + c, 2048, 16), V("ft", a, a + 4 * n - 3, 4), V("ft", a + 4 * n, a + 8 * n - 3, 4), 0.0, A.add, A.add)

    def quant_half(h):
        quant("qx", "sx", H * h, H * (h + 1), V("xt", 4 * H * h, 4 * H * (h + 1)))

    def unpack(b):
        mm(4 + b, QE, 128 * b, QX, 0, C)

    def old(b, a=0, z=FAR + 1, step=1):
        name, at = ("wn", WN * b + K) if b < 2 else ("th", OLD * (b - 2))
        return V(name, at + a, at + z, step)

    def pack(name, b):
        return V(name, K * b, K * b + K)

    for t in range(R):
        first = late if t == 0 else (lambda part: None)
        quant_half(0)
        quant_half(1)
        mm(3, QR, 0, QX, 0, H)
        mm(7, QR, 0, QX, H, H)
        mm(2, QU, 0, QX, 0, C)
        mm(0, QR, 0, QX, 0, C)
        mm(1, QR, 0, QX, 0, C)
        first("block ones")
        tt(V("u1", 0, H), bank(3, 0, H), V("k1", 0, H), A.subtract)
        tt(V("u1", H, C), bank(7, 0, H), V("k1", 0, H), A.subtract)
        for b in range(4 if t > 0 else 0):
            unpack(b)
        act(V("bw"), bank(2, 0, C), F.Sign, bias=NT, scale=KEEP)
        scan(V("z", 0, H), V("d0"), V("u1", 0, H), 0.0, A.add, A.max)
        scan(V("z", H, C), V("d0"), V("u1", H, C), 0.0, A.add, A.max)
        act(V("gm"), by(V("bw"), V("m16")))
        rows = [dma("y", lane("gm", 14), lane("lr", 14)), dma("y", lane("gm", 15), lane("mr", 15))]
        if t == 0:
            send(0, rows)
            select(V("g0t", 0, 512, 4), [[0, 8], [1, 16]], float(UNIT))
            iota(V("jy", 0, C), [[-1, C]], C)
            iota(V("jy", C, FAR + 1), [[1, C + 1]], 0)
            iota(V("ee"), [[0, SEG * KB]], 2)
        iota(V("ww", 0, C), [[1, C]], K)
        if t == 0:
            for b in range(2):
                zero("g", V("wz", W * b + K, W * b + W))
            send(1)
            send(2)
        for x in range(len(ON_SCALAR) + 1):
            if x < len(ON_SCALAR):
                n = 16 * ON_SCALAR[x]
                act(V("sgn", C * x, C * x + n), bank(1, 0, n), F.Sign, bias=col("z", n + 15), scale=-1.0)
            if x > 0:
                c = ON_SCALAR[x - 1]
                act(slot(c, 16 * c), V("sgn", C * (x - 1), C * (x - 1) + 16 * c), F.Relu, accum_out=col("rsb", c))
        for c in range(1, ON_SCALAR[-1]):
            ts(slot(c, 16 * c), bank(0, 0, 16 * c), col("z", 16 * c + 15), A.is_lt)
            if c == 3:
                tt(slot(NB, C), V("z"), bank(0, 0, C), A.is_ge)
            if c == 6:
                scan(V("dsum"), V("m0"), slot(NB, C), 0.0, A.mult, A.add)
                first("places")
            if c == 9:
                tt(V("r1"), V("rc"), V("dsum", 15, C, 16), A.subtract)
            if c == 10:
                first("ones")
                qtile(3, 5)
                sum_tile(4, first=True)
                sum_tile(3)
        for c in range(1, SUM_V):
            act(slot(c, 16 * c, "junk"), slot(c, 16 * c), F.Identity, accum_out=col("rsb", c))
        row_sum(SUM_V)
        for h in (2, 0, 1):
            qtile(h, h + 1)
            sum_tile(h, last=h == 1)
        for c in range(SUM_V + 1, ON_SCALAR[-1]):
            row_sum(c)
        tt(V("pp", 0, K), by(V("bw"), V("l16", 0, KB)), V("gm", 0, K), A.subtract)
        mine = V("r1", SUM_V, ON_SCALAR[-1])
        tt(mine, mine, V("vj", 2032 + SUM_V, 2032 + ON_SCALAR[-1]), A.subtract)
        first("lists")
        scan(V("rsc"), bank(3, 0, C), V("c16"), float(LIFT), A.min, A.add)
        tt(V("r2"), V("r1"), V("rsb"), A.subtract)
        tt(V("pp", K, C), by(V("bw"), V("l16", KB, NB)), V("gm", K, C), A.subtract)
        first(2)
        tt(V("pos"), V("rsc", 15, C, 16), V("r2"), A.add)
        first(3)
        cp(by(V("win"), V("pos")), V("pp"))
        first(0)
        turn(V("tr", 0, K), V("win", 0, K))
        first("signs")
        turn(V("tr", K, 2 * K), V("win", 16, 16 + K))
        first(1)
        first("firsts")
        for b in (2, 3, 0, 1):
            act(old(b, 0, C), bank(4 + b, 0, C))
            act(old(b, FAR, C, -1), bank(4 + b, 0, C))
        cp(V("tl", 0, 384, 4), by(V("tr"), V("g1l")))
        first("group 0")
        quant("ql", "sl", 0, 128, V("tl"))
        ts(V("y1", 8, 256, 16), by(V("tr"), V("g2l", 0, 1)), FAR - 160.0, A.add)
        ts(V("low"), by(V("tr"), V("g2l", 2, 3)), 160.0, A.add)
        mm(0, QG, 0, QL, 0, 128)
        tt(V("both"), V("y1", 8, 256, 16), V("low"), A.add)
        if t == 1:
            quant("qv", "sv", 0, 128, V("vt"))
        tt(V("y0", 1, 192, 2), bank(0, 0, 96), V("tl", 0, 384, 4), A.mult)
        scan(V("ys"), V("y0"), V("y1", 0, 192), 0.0, A.add, A.min)
        left, right = V("lf16", 0, KB), V("rt16", 0, KB)
        tt(left, V("ys", 8, 192, 16), V("low", 0, KB), A.max)
        tt(V("lrf", 0, KB), V("ys", 8, 192, 16), V("low", 0, KB), A.max)
        act(pack("gl", 0), by(old(0), left))
        act(V("fold", 0, KB), V("lrf", 0, KB), F.Abs, bias=-float(C))
        act(pack("gl", 1), by(old(1), left))
        act(V("ee", SEG - 1, SEG * KB, SEG), V("fold", 0, KB), F.Identity, scale=1.0 / 1024, bias=(160.0 - C) / 1024)
        act(pack("gl", 2), by(old(2), left))
        cp(pack("gl", 3), by(old(3), left))
        tt(right, V("both", 0, KB), V("lrf", 0, KB), A.subtract)
        cp(V("rowl"), by(V("jy"), left))
        for h in range(PARTS - 1, -1, -1):
            for c in range(HB * h, HB * h + HB):
                act(V("ee", SEG * (c + 1) - 1 - SEG_W[c], SEG * (c + 1) - 1), V("rowl", 16 * HB * h, 16 * (c + 1)), F.Abs,
                    bias=col("fold", c), scale=-1.0)
        for b in (3, 0, 1, 2):
            tt(V("mt", b, 4 * K, 4), by(old(b), right), pack("gl", b), A.subtract)

        def firsts(h0, h1):
            a, b = SEG * HB * h0, SEG * HB * h1
            scan(V("es", a, b), V("md", a, b), V("ee", a, b), 2.0, A.add, A.min)

        def places(h0, h1):
            ts(V("o16", HB * h0, HB * h1), V("es", SEG * (HB * h0 + 1) - 1, SEG * HB * h1, SEG), -1024.0, A.mult, 160.0, A.add)

        def put(h):
            cp(by(V("ww"), V("o16", HB * h, HB * h + HB)), V("jj", 16 * HB * h, 16 * HB * (h + 1)))

        def new(b):
            tt(V("wn", WN * b, WN * b + K), bank(4 + b, 0, K), pack("gl", b), A.add)

        firsts(1, 3)
        quant("qm", "sm", 0, K, V("mt"))
        for b in range(4):
            mm(b, ("lq%d" % t, "lp%d" % t), 128 * b, QM, 0, K, ext=[("arr%d" % t, lands[t])] if b == 0 else ())
        places(1, 3)
        firsts(0, 1)
        put(2)
        places(0, 1)
        for b in range(3):
            act(V("ht", b, 4 * K, 4), bank(b, 0, K), scale=0.03125)
        for b in (2, 3):
            act(V("tf", C * (b - 2), C * (b - 1)), old(b, 0, C), scale=-2.0)
        if t == R - 1:
            act(V("olr", 0, K), V("rowl"), F.Identity, scale=-1.0, bias=float(C))
            act(V("olr", K, 2 * K), by(V("jy"), right), F.Identity, scale=-1.0, bias=float(C))
            dma("y", T.ol[:], lane("olr", 0))
        put(1)
        ts(V("ht", 3, 4 * K, 4), bank(3, 0, K), 0.03125, A.mult)
        put(0)
        quant("qh", "sh", 0, K, V("ht"))
        for b in (2, 0, 3, 1):
            mm(4 + b, QE, 128 * b, QH, 0, K)
        scan(V("wsc"), V("ww", 0, C), V("c16"), float(LIFT), A.min, A.add)
        for b in (2, 3):
            act(V("wz", W * (b - 2), W * (b - 2) + K), bank(4 + b, 0, K), scale=-2.0)
        ts(V("who"), V("wsc", 15, C, 16), WF, A.add)
        new(0)
        new(1)
        for b in (0, 1):
            act(V("xt", b, 4 * C, 4), by(V("wn", WN * b, WN * b + W), V("who")), scale=-2.0)
        for b in (2, 3):
            tt(V("xt", b, 4 * C, 4), by(V("wz", W * (b - 2), W * (b - 1)), V("who")), V("tf", C * (b - 2), C * (b - 1)), A.add)

    quant_half(0)
    quant_half(1)
    mm(0, QV, 0, QX, 0, H)
    mm(1, QV, 0, QX, H, H)
    dma("s", T.oc[:, 0:4 * H], as_(V("qx", 0, H), dt.uint8))
    dma("y", T.oc[:, 4 * H:4 * C], as_(V("qx", H, C), dt.uint8))
    for k in range(4):
        dma("y", T.osc[4 * k:4 * k + 4, :], V("sx", parts=slice(32 * k, 32 * k + 4)))
    cp(V("ysb", 0, H), bank(0, 0, H))
    act(V("ysb", H, C), bank(1, 0, H))
    dma("y", T.y[:, 0:H], V("ysb", 0, H))
    dma("s", T.y[:, H:C], V("ysb", H, C))
    plan(g, T, ops)
    g.wait_ge(T.sem.sent, sent[0])
